import numpy as np
import ml_dtypes


def mxq(x, axis, fmt="e4m3"):
    dtype, down = {"e4m3": (ml_dtypes.float8_e4m3fn, 7), "e5m2": (ml_dtypes.float8_e5m2, 14)}[fmt]
    v = np.moveaxis(np.asarray(x, np.float32).astype(ml_dtypes.bfloat16).astype(np.float64), axis, -1)
    blocks = v.reshape(v.shape[:-1] + (-1, 32))
    amax = np.abs(blocks).max(-1, keepdims=True)
    byte = np.maximum(np.where(amax > 0, np.frexp(amax)[1] - 1 + 127, 0) - down, 1)
    scale = np.exp2(byte - 127.0)
    codes = (blocks / scale).astype(np.float32).astype(dtype).astype(np.float64)
    return np.moveaxis((codes * scale).reshape(v.shape), -1, axis)


WIDE = False


def mx_kscale(k):
    if not WIDE:
        return np.ones(k)
    levels = np.array([10, -10, 5, -5, 0])
    if k % 512:
        return np.exp2(np.random.permutation(np.resize(levels, k // 32))).repeat(32)
    a = np.empty((k // 512, 16))
    for p in range(k // 512):
        a[p, :8] = np.random.permutation(np.resize(levels, 8))
        for g in range(8):
            far = levels[np.abs(levels - a[p, g]) >= 10]
            a[p, g + 8] = far[np.random.randint(len(far))]
    return np.exp2(a.ravel()).repeat(32)


def f64(x):
    return np.asarray(x).astype(np.float64)


def striped(idx):
    return np.tile(idx.reshape(-1, 16).T, (8, 1)).astype(np.uint16)


def unstriped(offs):
    return offs[:16].T.reshape(-1).astype(np.int64)


K, T, E, C, N = 2048, 512, 2, 256, 128


def by_expert(wq, xq):
    return np.concatenate([wq[e].T @ xq[:, e * C:(e + 1) * C] for e in range(E)], axis=1)


def setup_inputs():
    n = np.random.standard_normal
    s = mx_kscale(K)[:, None]
    return {
        "xT": (n((K, T)) * s).astype(np.float32),
        "w": (n((E, K, N)) / np.sqrt(K) / s[None]).astype(np.float32),
        "gate": np.tile(np.random.uniform(0.2, 1.0, E * C), (N, 1)).astype(np.float32),
        "offs": striped(np.random.permutation(T)[:E * C]),
    }


def reference(xT, w, gate, offs):
    idx = unstriped(offs)
    xq = mxq(f64(xT)[:, idx], 0, "e4m3")
    y = by_expert(mxq(f64(w), 1, "e4m3"), xq)
    out = np.zeros((N, T))
    out[:, idx] = f64(gate) * y
    return out

@@ -1,0 +1,139 @@
+from contextlib import ExitStack
+
+import concourse.mybir as mybir
+
+K, T, E, C, N = 2048, 512, 2, 256, 128
+FLOPS = 2 * K * N * E * C
+
+F32 = mybir.dt.float32
+BF16 = mybir.dt.bfloat16
+U32 = mybir.dt.uint32
+U16 = mybir.dt.uint16
+U8 = mybir.dt.uint8
+FP8X4 = mybir.dt.float8_e4m3fn_x4
+
+P = 128
+PACK = 4
+K_PASS = P * PACK
+PASSES = K // K_PASS
+LIST_COLS = C // 16
+
+UNITS = [(0, 0), (0, 1), (1, 0), (1, 1), (2, 0), (3, 0), (2, 1), (3, 1)]
+
+
+def tile_routed_moe_kernel(tc, xT, w, gate, offs, out):
+    nc = tc.nc
+    mult = mybir.AluOpType.mult
+    x_planes = xT.rearrange("(g p t) n -> g p t n", p=P, t=PACK)
+    w_passes = w.rearrange("e (g p j) n -> g p e j n", p=P, j=PACK)
+
+    with ExitStack() as ctx:
+        lists = ctx.enter_context(tc.tile_pool(name="lists", bufs=1))
+        held = ctx.enter_context(tc.tile_pool(name="held", bufs=1))
+        psum = ctx.enter_context(tc.psum_pool(name="psum", bufs=1))
+
+        offsets = lists.tile([P, E * C // 16], U16, name="offsets")
+        nc.sync.dma_start(offsets[:], offs)
+
+        planes = {}
+        w_raw = {}
+        for g in range(PASSES):
+            for t in range(PACK):
+                planes[(g, t)] = held.tile([P, T], F32, name="plane_%d_%d" % (g, t))
+                nc.sync.dma_start(planes[(g, t)][:], x_planes[g, :, t, :])
+            w_raw[g] = held.tile([P, E, PACK, N], F32, name="w_raw_%d" % g)
+            nc.sync.dma_start(w_raw[g][:], w_passes[g])
+        gate_sb = held.tile([P, E * C], F32, name="gate_sb")
+        nc.sync.dma_start(gate_sb[:], gate)
+
+        acc = [psum.tile([N, C], F32, name="acc_%d" % e) for e in range(E)]
+        result = held.tile([N, T], F32, name="result")
+
+        gathered = {}
+        x_bf = {}
+        x_codes = {}
+        x_scales = {}
+        w_bf = {}
+        w_codes = {}
+        w_scales = {}
+
+        def slot_list(e):
+            return offsets[:, e * LIST_COLS : (e + 1) * LIST_COLS]
+
+        def gather(u):
+            g, e = u
+            gathered[u] = held.tile([P, PACK, C], F32, name="gathered_%d_%d" % u)
+            for t in range(PACK):
+                nc.vector.tensor_copy(gathered[u][:, t, :], planes[(g, t)][:].indirect(slot_list(e)))
+
+        def interleave(u):
+            x_bf[u] = held.tile([P, C, PACK], BF16, name="x_bf_%d_%d" % u, align_bytes=64)
+            nc.scalar.copy(x_bf[u][:], gathered[u][:].rearrange("p t c -> p c t"))
+
+        def quantize(u):
+            x_codes[u] = held.tile([P, C], U32, name="x_codes_%d_%d" % u, align_bytes=64)
+            x_scales[u] = held.tile([P, C], U8, name="x_scales_%d_%d" % u, align_bytes=64)
+            nc.vector.quantize_mx(
+                out=x_codes[u][:].bitcast(FP8X4),
+                scales=x_scales[u][:],
+                in_=x_bf[u][:].rearrange("p c t -> p (c t)"),
+            )
+
+        def w_interleave(g):
+            w_bf[g] = held.tile([P, E, N, PACK], BF16, name="w_bf_%d" % g, align_bytes=64)
+            nc.scalar.copy(w_bf[g][:], w_raw[g][:].rearrange("p e j n -> p e n j"))
+
+        def w_quantize(g):
+            w_codes[g] = held.tile([P, E * N], U32, name="w_codes_%d" % g, align_bytes=64)
+            w_scales[g] = held.tile([P, E * N], U8, name="w_scales_%d" % g, align_bytes=64)
+            nc.vector.quantize_mx(
+                out=w_codes[g][:].bitcast(FP8X4),
+                scales=w_scales[g][:],
+                in_=w_bf[g][:].rearrange("p e n j -> p (e n j)"),
+            )
+
+        def multiply(u):
+            g, e = u
+            cols = slice(e * N, (e + 1) * N)
+            nc.tensor.matmul_mx(
+                out=acc[e][:],
+                lhsT=w_codes[g][:, cols].bitcast(FP8X4),
+                lhsT_scale=w_scales[g][:, cols],
+                rhs=x_codes[u][:].bitcast(FP8X4),
+                rhs_scale=x_scales[u][:],
+                start=(g == 0),
+                stop=(g == PASSES - 1),
+            )
+
+        sums = {}
+
+        def empty_bank(e):
+            sums[e] = held.tile([N, C], F32, name="sums_%d" % e)
+            nc.scalar.copy(sums[e][:], acc[e][:])
+
+        def scatter(e):
+            nc.vector.tensor_tensor(
+                result[:].indirect(slot_list(e)), sums[e][:], gate_sb[:, e * C : (e + 1) * C], mult
+            )
+
+        def finish(u):
+            g, e = u
+            if g not in w_codes:
+                w_quantize(g)
+            quantize(u)
+            multiply(u)
+            if g == PASSES - 1:
+                empty_bank(e)
+
+        for i, u in enumerate(UNITS):
+            gather(u)
+            interleave(u)
+            if u[0] not in w_bf:
+                w_interleave(u[0])
+            if i >= 1:
+                finish(UNITS[i - 1])
+        scatter(0)
+        finish(UNITS[-1])
+        scatter(1)
+
+        nc.sync.dma_start(out, result[:])

@@ -17,13 +17,16 @@ PACK = 4
 K_PASS = P * PACK
 PASSES = K // K_PASS
 LIST_COLS = C // 16
+WINDOW = 2048
 
-UNITS = [(0, 0), (0, 1), (1, 0), (1, 1), (2, 0), (3, 0), (2, 1), (3, 1)]
+PF, PA, PG, PB = 0, 1, 2, 3
+ORDER = [PF, PA, PG, PB]
 
 
 def tile_routed_moe_kernel(tc, xT, w, gate, offs, out):
     nc = tc.nc
     mult = mybir.AluOpType.mult
+    copy_fn = mybir.ActivationFunctionType.Copy
     x_planes = xT.rearrange("(g p t) n -> g p t n", p=P, t=PACK)
     w_passes = w.rearrange("e (g p j) n -> g p e j n", p=P, j=PACK)
 
@@ -36,11 +39,23 @@ def tile_routed_moe_kernel(tc, xT, w, gate, offs, out):
         nc.sync.dma_start(offsets[:], offs)
 
         planes = {}
+        raw = {}
+        raw_bf = {}
         w_raw = {}
-        for g in range(PASSES):
+        for g in (PF, PG):
+            raw[g] = held.tile([P, PACK, T], F32, name="raw_%d" % g)
+            raw_bf[g] = held.tile([P, PACK, T], BF16, name="raw_bf_%d" % g)
+        for g in (PA, PB):
             for t in range(PACK):
-                planes[(g, t)] = held.tile([P, T], F32, name="plane_%d_%d" % (g, t))
-                nc.sync.dma_start(planes[(g, t)][:], x_planes[g, :, t, :])
+                planes[(g, t)] = held.tile([P, WINDOW], F32, name="plane_%d_%d" % (g, t))
+
+        for t in range(PACK):
+            nc.sync.dma_start(raw[PF][:, t, :], x_planes[PF, :, t, :])
+            nc.sync.dma_start(planes[(PA, t)][:, 0:T], x_planes[PA, :, t, :])
+        nc.sync.dma_start(raw[PG][:], x_planes[PG])
+        for t in range(PACK):
+            nc.sync.dma_start(planes[(PB, t)][:, 0:T], x_planes[PB, :, t, :])
+        for g in range(PASSES):
             w_raw[g] = held.tile([P, E, PACK, N], F32, name="w_raw_%d" % g)
             nc.sync.dma_start(w_raw[g][:], w_passes[g])
         gate_sb = held.tile([P, E * C], F32, name="gate_sb")
@@ -56,32 +71,48 @@ def tile_routed_moe_kernel(tc, xT, w, gate, offs, out):
         w_bf = {}
         w_codes = {}
         w_scales = {}
+        sums = {}
+        for g in range(PASSES):
+            x_bf[g] = held.tile([P, E * C, PACK], BF16, name="x_bf_%d" % g, align_bytes=64)
+            x_codes[g] = held.tile([P, E * C], U32, name="x_codes_%d" % g, align_bytes=64)
+            x_scales[g] = held.tile([P, E * C], U8, name="x_scales_%d" % g, align_bytes=64)
+        for g in (PA, PB):
+            gathered[g] = held.tile([P, PACK, E * C], F32, name="gathered_%d" % g)
 
         def slot_list(e):
             return offsets[:, e * LIST_COLS : (e + 1) * LIST_COLS]
 
-        def gather(u):
-            g, e = u
-            gathered[u] = held.tile([P, PACK, C], F32, name="gathered_%d_%d" % u)
-            for t in range(PACK):
-                nc.vector.tensor_copy(gathered[u][:, t, :], planes[(g, t)][:].indirect(slot_list(e)))
+        def slots(e):
+            return slice(e * C, (e + 1) * C)
 
-        def interleave(u):
-            x_bf[u] = held.tile([P, C, PACK], BF16, name="x_bf_%d_%d" % u, align_bytes=64)
-            nc.scalar.copy(x_bf[u][:], gathered[u][:].rearrange("p t c -> p c t"))
+        def cast(g, t):
+            nc.vector.tensor_copy(raw_bf[g][:, t, :], raw[g][:, t, :])
 
-        def quantize(u):
-            x_codes[u] = held.tile([P, C], U32, name="x_codes_%d_%d" % u, align_bytes=64)
-            x_scales[u] = held.tile([P, C], U8, name="x_scales_%d_%d" % u, align_bytes=64)
+        def cast_all(g):
+            nc.vector.tensor_copy(raw_bf[g][:], raw[g][:])
+
+        def scalar_gather(g, t, e):
+            nc.scalar.activation(x_bf[g][:, slots(e), t], raw_bf[g][:, t, :].indirect(slot_list(e)), copy_fn)
+
+        def gather_all(g, t):
+            nc.vector.tensor_copy(gathered[g][:, t, :], planes[(g, t)][:].indirect(offsets[:]))
+
+        def gather(g, t, e):
+            nc.vector.tensor_copy(gathered[g][:, t, slots(e)], planes[(g, t)][:].indirect(slot_list(e)))
+
+        def interleave(g, e):
+            nc.scalar.copy(x_bf[g][:, slots(e), :], gathered[g][:, :, slots(e)].rearrange("p t c -> p c t"))
+
+        def quantize(g, cols):
             nc.vector.quantize_mx(
-                out=x_codes[u][:].bitcast(FP8X4),
-                scales=x_scales[u][:],
-                in_=x_bf[u][:].rearrange("p c t -> p (c t)"),
+                out=x_codes[g][:, cols].bitcast(FP8X4),
+                scales=x_scales[g][:, cols],
+                in_=x_bf[g][:, cols, :].rearrange("p c t -> p (c t)"),
             )
 
         def w_interleave(g):
             w_bf[g] = held.tile([P, E, N, PACK], BF16, name="w_bf_%d" % g, align_bytes=64)
-            nc.scalar.copy(w_bf[g][:], w_raw[g][:].rearrange("p e j n -> p e n j"))
+            nc.vector.tensor_copy(w_bf[g][:], w_raw[g][:].rearrange("p e j n -> p e n j"))
 
         def w_quantize(g):
             w_codes[g] = held.tile([P, E * N], U32, name="w_codes_%d" % g, align_bytes=64)
@@ -92,48 +123,59 @@ def tile_routed_moe_kernel(tc, xT, w, gate, offs, out):
                 in_=w_bf[g][:].rearrange("p e n j -> p (e n j)"),
             )
 
-        def multiply(u):
-            g, e = u
+        def multiply(g, e):
             cols = slice(e * N, (e + 1) * N)
             nc.tensor.matmul_mx(
                 out=acc[e][:],
                 lhsT=w_codes[g][:, cols].bitcast(FP8X4),
                 lhsT_scale=w_scales[g][:, cols],
-                rhs=x_codes[u][:].bitcast(FP8X4),
-                rhs_scale=x_scales[u][:],
-                start=(g == 0),
-                stop=(g == PASSES - 1),
+                rhs=x_codes[g][:, slots(e)].bitcast(FP8X4),
+                rhs_scale=x_scales[g][:, slots(e)],
+                start=(g == ORDER[0]),
+                stop=(g == ORDER[-1]),
             )
-
-        sums = {}
 
         def empty_bank(e):
             sums[e] = held.tile([N, C], F32, name="sums_%d" % e)
             nc.scalar.copy(sums[e][:], acc[e][:])
 
         def scatter(e):
-            nc.vector.tensor_tensor(
-                result[:].indirect(slot_list(e)), sums[e][:], gate_sb[:, e * C : (e + 1) * C], mult
-            )
+            nc.vector.tensor_tensor(result[:].indirect(slot_list(e)), sums[e][:], gate_sb[:, slots(e)], mult)
 
-        def finish(u):
-            g, e = u
-            if g not in w_codes:
-                w_quantize(g)
-            quantize(u)
-            multiply(u)
-            if g == PASSES - 1:
-                empty_bank(e)
+        warm = held.tile([P, 1], F32, name="warm")
+        nc.vector.memset(warm[:], 0.0)
+        warm_out = held.tile([P, 1], F32, name="warm_out")
+        nc.scalar.activation(warm_out[:], warm[:], copy_fn)
 
-        for i, u in enumerate(UNITS):
-            gather(u)
-            interleave(u)
-            if u[0] not in w_bf:
-                w_interleave(u[0])
-            if i >= 1:
-                finish(UNITS[i - 1])
-        scatter(0)
-        finish(UNITS[-1])
-        scatter(1)
+        every = slice(0, E * C)
+        for t in range(PACK):
+            cast(PF, t)
+            scalar_gather(PF, t, 0)
+            scalar_gather(PF, t, 1)
+            gather_all(PA, t)
+        interleave(PA, 0)
+        interleave(PA, 1)
+        cast_all(PG)
+        for e in range(E):
+            for t in range(PACK):
+                scalar_gather(PG, t, e)
+        for t in range(PACK):
+            gather_all(PB, t)
+        interleave(PB, 0)
+        interleave(PB, 1)
+        for g in ORDER:
+            w_interleave(g)
+        for g in ORDER:
+            w_quantize(g)
+        for g in (PF, PA, PG):
+            quantize(g, every)
+            multiply(g, 0)
+            multiply(g, 1)
+        for e in range(E):
+            quantize(PB, slots(e))
+            multiply(PB, e)
+            empty_bank(e)
+        for e in range(E):
+            scatter(e)
 
         nc.sync.dma_start(out, result[:])

@@ -14,13 +14,13 @@ FP8X4 = mybir.dt.float8_e4m3fn_x4
 
 P = 128
 PACK = 4
-K_PASS = P * PACK
-PASSES = K // K_PASS
-LIST_COLS = C // 16
+PASSES = K // (P * PACK)
+SLOTS = E * C
 WINDOW = 2048
 
-PF, PA, PG, PB = 0, 1, 2, 3
-ORDER = [PF, PA, PG, PB]
+FIRST_S, FIRST_V, SECOND_V, SECOND_S = 0, 1, 2, 3
+W_GROUPS = ((0, 1), (2, 3))
+GROUPS = ((0, 256), (256, 384), (384, 512))
 
 
 def tile_routed_moe_kernel(tc, xT, w, gate, offs, out):
@@ -35,147 +35,153 @@ def tile_routed_moe_kernel(tc, xT, w, gate, offs, out):
         held = ctx.enter_context(tc.tile_pool(name="held", bufs=1))
         psum = ctx.enter_context(tc.psum_pool(name="psum", bufs=1))
 
-        offsets = lists.tile([P, E * C // 16], U16, name="offsets")
+        offsets = lists.tile([P, SLOTS // 16], U16, name="offsets")
         nc.sync.dma_start(offsets[:], offs)
-
-        planes = {}
-        raw = {}
-        raw_bf = {}
-        w_raw = {}
-        for g in (PF, PG):
-            raw[g] = held.tile([P, PACK, T], F32, name="raw_%d" % g)
-            raw_bf[g] = held.tile([P, PACK, T], BF16, name="raw_bf_%d" % g)
-        for g in (PA, PB):
-            for t in range(PACK):
-                planes[(g, t)] = held.tile([P, WINDOW], F32, name="plane_%d_%d" % (g, t))
-
-        for t in range(PACK):
-            nc.sync.dma_start(raw[PF][:, t, :], x_planes[PF, :, t, :])
-            nc.sync.dma_start(planes[(PA, t)][:, 0:T], x_planes[PA, :, t, :])
-        nc.sync.dma_start(raw[PG][:], x_planes[PG])
-        for t in range(PACK):
-            nc.sync.dma_start(planes[(PB, t)][:, 0:T], x_planes[PB, :, t, :])
-        for g in range(PASSES):
-            w_raw[g] = held.tile([P, E, PACK, N], F32, name="w_raw_%d" % g)
-            nc.sync.dma_start(w_raw[g][:], w_passes[g])
-        gate_sb = held.tile([P, E * C], F32, name="gate_sb")
-        nc.sync.dma_start(gate_sb[:], gate)
-
-        acc = [psum.tile([N, C], F32, name="acc_%d" % e) for e in range(E)]
-        result = held.tile([N, T], F32, name="result")
-
-        gathered = {}
-        x_bf = {}
-        x_codes = {}
-        x_scales = {}
-        w_bf = {}
-        w_codes = {}
-        w_scales = {}
-        sums = {}
-        for g in range(PASSES):
-            x_bf[g] = held.tile([P, E * C, PACK], BF16, name="x_bf_%d" % g, align_bytes=64)
-            x_codes[g] = held.tile([P, E * C], U32, name="x_codes_%d" % g, align_bytes=64)
-            x_scales[g] = held.tile([P, E * C], U8, name="x_scales_%d" % g, align_bytes=64)
-        for g in (PA, PB):
-            gathered[g] = held.tile([P, PACK, E * C], F32, name="gathered_%d" % g)
-
-        def slot_list(e):
-            return offsets[:, e * LIST_COLS : (e + 1) * LIST_COLS]
-
-        def slots(e):
-            return slice(e * C, (e + 1) * C)
-
-        def cast(g, t):
-            nc.vector.tensor_copy(raw_bf[g][:, t, :], raw[g][:, t, :])
-
-        def cast_all(g):
-            nc.vector.tensor_copy(raw_bf[g][:], raw[g][:])
-
-        def scalar_gather(g, t, e):
-            nc.scalar.activation(x_bf[g][:, slots(e), t], raw_bf[g][:, t, :].indirect(slot_list(e)), copy_fn)
-
-        def gather_all(g, t):
-            nc.vector.tensor_copy(gathered[g][:, t, :], planes[(g, t)][:].indirect(offsets[:]))
-
-        def gather(g, t, e):
-            nc.vector.tensor_copy(gathered[g][:, t, slots(e)], planes[(g, t)][:].indirect(slot_list(e)))
-
-        def interleave(g, e):
-            nc.scalar.copy(x_bf[g][:, slots(e), :], gathered[g][:, :, slots(e)].rearrange("p t c -> p c t"))
-
-        def quantize(g, cols):
-            nc.vector.quantize_mx(
-                out=x_codes[g][:, cols].bitcast(FP8X4),
-                scales=x_scales[g][:, cols],
-                in_=x_bf[g][:, cols, :].rearrange("p c t -> p (c t)"),
-            )
-
-        def w_interleave(g):
-            w_bf[g] = held.tile([P, E, N, PACK], BF16, name="w_bf_%d" % g, align_bytes=64)
-            nc.vector.tensor_copy(w_bf[g][:], w_raw[g][:].rearrange("p e j n -> p e n j"))
-
-        def w_quantize(g):
-            w_codes[g] = held.tile([P, E * N], U32, name="w_codes_%d" % g, align_bytes=64)
-            w_scales[g] = held.tile([P, E * N], U8, name="w_scales_%d" % g, align_bytes=64)
-            nc.vector.quantize_mx(
-                out=w_codes[g][:].bitcast(FP8X4),
-                scales=w_scales[g][:],
-                in_=w_bf[g][:].rearrange("p e n j -> p (e n j)"),
-            )
-
-        def multiply(g, e):
-            cols = slice(e * N, (e + 1) * N)
-            nc.tensor.matmul_mx(
-                out=acc[e][:],
-                lhsT=w_codes[g][:, cols].bitcast(FP8X4),
-                lhsT_scale=w_scales[g][:, cols],
-                rhs=x_codes[g][:, slots(e)].bitcast(FP8X4),
-                rhs_scale=x_scales[g][:, slots(e)],
-                start=(g == ORDER[0]),
-                stop=(g == ORDER[-1]),
-            )
-
-        def empty_bank(e):
-            sums[e] = held.tile([N, C], F32, name="sums_%d" % e)
-            nc.scalar.copy(sums[e][:], acc[e][:])
-
-        def scatter(e):
-            nc.vector.tensor_tensor(result[:].indirect(slot_list(e)), sums[e][:], gate_sb[:, slots(e)], mult)
 
         warm = held.tile([P, 1], F32, name="warm")
         nc.vector.memset(warm[:], 0.0)
         warm_out = held.tile([P, 1], F32, name="warm_out")
         nc.scalar.activation(warm_out[:], warm[:], copy_fn)
 
-        every = slice(0, E * C)
-        for t in range(PACK):
-            cast(PF, t)
-            scalar_gather(PF, t, 0)
-            scalar_gather(PF, t, 1)
-            gather_all(PA, t)
-        interleave(PA, 0)
-        interleave(PA, 1)
-        cast_all(PG)
-        for e in range(E):
+        raw = {}
+        raw_bf = {}
+        planes = {}
+        gathered = {}
+        x_bf = {}
+        for g in (FIRST_S, SECOND_S):
+            raw[g] = held.tile([P, PACK, T], F32, name="raw_%d" % g)
+            raw_bf[g] = held.tile([P, PACK, T], BF16, name="raw_bf_%d" % g)
+        for g in (FIRST_V, SECOND_V):
+            gathered[g] = held.tile([P, PACK, SLOTS], F32, name="gathered_%d" % g)
             for t in range(PACK):
-                scalar_gather(PG, t, e)
+                planes[(g, t)] = held.tile([P, WINDOW], F32, name="plane_%d_%d" % (g, t))
+        for g in range(PASSES):
+            x_bf[g] = held.tile([P, SLOTS, PACK], BF16, name="x_bf_%d" % g, align_bytes=64)
+        w_raw = [
+            held.tile([P, 2, E, PACK, N], F32, name="w_raw_%d" % i, tag="raw_then_codes_%d" % i, align_bytes=64)
+            for i in range(2)
+        ]
+        w_bf = [
+            held.tile([P, 2, E, N, PACK], BF16, name="w_bf_%d" % i, tag="bf_then_codes_%d" % i, align_bytes=64)
+            for i in range(2)
+        ]
+        w_codes = [held.tile([P, 2 * E * N], U32, name="w_codes_%d" % i, align_bytes=64) for i in range(2)]
+        w_scales = [held.tile([P, 2 * E * N], U8, name="w_scales_%d" % i, align_bytes=64) for i in range(2)]
+        gate_sb = held.tile([P, SLOTS], F32, name="gate_sb")
+        result = held.tile([N, T], F32, name="result")
+
+        def load_plane(g, t):
+            if g in raw:
+                nc.sync.dma_start(raw[g][:, t, :], x_planes[g, :, t, :])
+            else:
+                nc.sync.dma_start(planes[(g, t)][:, 0:T], x_planes[g, :, t, :])
+
+        for g, t in ((1, 0), (0, 0), (1, 1), (0, 1), (1, 2), (0, 2), (0, 3), (1, 3), (2, 0), (2, 1), (2, 2), (2, 3)):
+            load_plane(g, t)
+        nc.sync.dma_start(raw[SECOND_S][:], x_planes[SECOND_S])
+        for g in range(PASSES):
+            nc.sync.dma_start(w_raw[g // 2][:, g % 2], w_passes[g])
+        nc.sync.dma_start(gate_sb[:], gate)
+
+        acc = [psum.tile([N, hi - lo], F32, name="acc_%d" % i) for i, (lo, hi) in enumerate(GROUPS)]
+        sums = [
+            held.tile([N, hi - lo], F32, name="sums_%d" % i, tag="sums_%d" % i, align_bytes=64)
+            for i, (lo, hi) in enumerate(GROUPS)
+        ]
+        x_scales = [held.tile([P, SLOTS], U8, name="x_scales_%d" % g, align_bytes=64) for g in range(PASSES)]
+        x_codes = {}
+
+        def slot_list(lo, hi):
+            return offsets[:, lo // 16 : hi // 16]
+
+        def scalar_gather(g, t, lo, hi):
+            nc.scalar.activation(x_bf[g][:, lo:hi, t], raw_bf[g][:, t, :].indirect(slot_list(lo, hi)), copy_fn)
+
+        def vector_gather(g, t):
+            nc.vector.tensor_copy(gathered[g][:, t, :], planes[(g, t)][:].indirect(offsets[:]))
+
+        def interleave(g, lo, hi):
+            nc.scalar.copy(x_bf[g][:, lo:hi, :], gathered[g][:, :, lo:hi].rearrange("p t c -> p c t"))
+
+        def quantize(g, lo, hi, codes, c0):
+            nc.vector.quantize_mx(
+                out=codes[:, lo - c0 : hi - c0].bitcast(FP8X4),
+                scales=x_scales[g][:, lo:hi],
+                in_=x_bf[g][:, lo:hi, :].rearrange("p c t -> p (c t)"),
+            )
+            x_codes[(g, lo)] = (codes, c0)
+
+        def w_interleave(i):
+            nc.vector.tensor_copy(
+                w_bf[i][:].rearrange("p g e n j -> p (g e) n j"), w_raw[i][:].rearrange("p g e j n -> p (g e) n j")
+            )
+
+        def w_quantize(i):
+            nc.vector.quantize_mx(
+                out=w_codes[i][:].bitcast(FP8X4),
+                scales=w_scales[i][:],
+                in_=w_bf[i][:].rearrange("p g e n j -> p (g e n j)"),
+            )
+
+        def multiply(g, i):
+            lo, hi = GROUPS[i]
+            codes, c0 = x_codes[(g, lo)] if (g, lo) in x_codes else x_codes[(g, 0)]
+            col = ((g % 2) * E + lo // C) * N
+            nc.tensor.matmul_mx(
+                out=acc[i][:],
+                lhsT=w_codes[g // 2][:, col : col + N].bitcast(FP8X4),
+                lhsT_scale=w_scales[g // 2][:, col : col + N],
+                rhs=codes[:, lo - c0 : hi - c0].bitcast(FP8X4),
+                rhs_scale=x_scales[g][:, lo:hi],
+                start=(g == 0),
+                stop=(g == PASSES - 1),
+            )
+
+        def scatter(i):
+            lo, hi = GROUPS[i]
+            nc.vector.tensor_tensor(result[:].indirect(slot_list(lo, hi)), sums[i][:], gate_sb[:, lo:hi], mult)
+
         for t in range(PACK):
-            gather_all(PB, t)
-        interleave(PB, 0)
-        interleave(PB, 1)
-        for g in ORDER:
-            w_interleave(g)
-        for g in ORDER:
-            w_quantize(g)
-        for g in (PF, PA, PG):
-            quantize(g, every)
-            multiply(g, 0)
-            multiply(g, 1)
-        for e in range(E):
-            quantize(PB, slots(e))
-            multiply(PB, e)
-            empty_bank(e)
-        for e in range(E):
-            scatter(e)
+            nc.scalar.copy(raw_bf[FIRST_S][:, t, :], raw[FIRST_S][:, t, :])
+            for e in range(E):
+                scalar_gather(FIRST_S, t, e * C, (e + 1) * C)
+        for g in (FIRST_V, SECOND_V):
+            for t in range(PACK):
+                vector_gather(g, t)
+        for g in (FIRST_V, SECOND_V):
+            for e in range(E):
+                interleave(g, e * C, (e + 1) * C)
+        nc.vector.tensor_copy(raw_bf[SECOND_S][:], raw[SECOND_S][:])
+        for lo, hi in GROUPS:
+            for t in range(PACK):
+                scalar_gather(SECOND_S, t, lo, hi)
+
+        w_interleave(0)
+        codes_0 = held.tile([P, SLOTS], U32, name="codes_0", tag="raw_then_codes_0", align_bytes=64)
+        quantize(0, 0, SLOTS, codes_0, 0)
+        w_quantize(0)
+        codes_1 = held.tile([P, SLOTS], U32, name="codes_1", tag="bf_then_codes_0", align_bytes=64)
+        quantize(1, 0, SLOTS, codes_1, 0)
+        w_interleave(1)
+        codes_2 = held.tile([P, SLOTS], U32, name="codes_2", tag="raw_then_codes_1", align_bytes=64)
+        w_quantize(1)
+        quantize(2, 0, SLOTS, codes_2, 0)
+        codes_3 = held.tile([P, GROUPS[1][1]], U32, name="codes_3", tag="bf_then_codes_1", align_bytes=64)
+
+        for i, (lo, hi) in enumerate(GROUPS):
+            if i == 2:
+                scatter(0)
+                codes_last = held.tile([P, hi - lo], U32, name="codes_last", tag="sums_0", align_bytes=64)
+                quantize(3, lo, hi, codes_last, lo)
+            else:
+                quantize(3, lo, hi, codes_3, 0)
+            for g in range(PASSES):
+                multiply(g, i)
+            if i == 0:
+                nc.vector.tensor_copy(sums[i][:], acc[i][:])
+            else:
+                nc.scalar.copy(sums[i][:], acc[i][:])
+        scatter(1)
+        scatter(2)
 
         nc.sync.dma_start(out, result[:])

@@ -16,10 +16,9 @@ P = 128
 PACK = 4
 PASSES = K // (P * PACK)
 SLOTS = E * C
-WINDOW = 2048
+WINDOW = 2 * T
 
 FIRST_S, FIRST_V, SECOND_V, SECOND_S = 0, 1, 2, 3
-W_GROUPS = ((0, 1), (2, 3))
 GROUPS = ((0, 256), (256, 384), (384, 512))
 
 
@@ -45,18 +44,16 @@ def tile_routed_moe_kernel(tc, xT, w, gate, offs, out):
 
         raw = {}
         raw_bf = {}
-        planes = {}
-        gathered = {}
         x_bf = {}
         for g in (FIRST_S, SECOND_S):
             raw[g] = held.tile([P, PACK, T], F32, name="raw_%d" % g)
             raw_bf[g] = held.tile([P, PACK, T], BF16, name="raw_bf_%d" % g)
         for g in (FIRST_V, SECOND_V):
-            gathered[g] = held.tile([P, PACK, SLOTS], F32, name="gathered_%d" % g)
-            for t in range(PACK):
-                planes[(g, t)] = held.tile([P, WINDOW], F32, name="plane_%d_%d" % (g, t))
-        for g in range(PASSES):
-            x_bf[g] = held.tile([P, SLOTS, PACK], BF16, name="x_bf_%d" % g, align_bytes=64)
+            raw[g] = held.tile([P, (PACK + 1) * T], F32, name="raw_%d" % g)
+        for g in (FIRST_S, FIRST_V, SECOND_V):
+            x_bf[(g, 0)] = held.tile([P, SLOTS, PACK], BF16, name="x_bf_%d" % g, align_bytes=64)
+        x_bf[(SECOND_S, 0)] = held.tile([P, C, PACK], BF16, name="x_bf_3a", tag="bf_then_codes_2", align_bytes=64)
+        x_bf[(SECOND_S, C)] = held.tile([P, C, PACK], BF16, name="x_bf_3b", align_bytes=64)
         w_raw = [
             held.tile([P, 2, E, PACK, N], F32, name="w_raw_%d" % i, tag="raw_then_codes_%d" % i, align_bytes=64)
             for i in range(2)
@@ -70,11 +67,14 @@ def tile_routed_moe_kernel(tc, xT, w, gate, offs, out):
         gate_sb = held.tile([P, SLOTS], F32, name="gate_sb")
         result = held.tile([N, T], F32, name="result")
 
+        def first_column(t):
+            return (PACK - 1 - t) * T
+
         def load_plane(g, t):
-            if g in raw:
+            if g in raw_bf:
                 nc.sync.dma_start(raw[g][:, t, :], x_planes[g, :, t, :])
             else:
-                nc.sync.dma_start(planes[(g, t)][:, 0:T], x_planes[g, :, t, :])
+                nc.sync.dma_start(raw[g][:, first_column(t) : first_column(t) + T], x_planes[g, :, t, :])
 
         for g, t in ((1, 0), (0, 0), (1, 1), (0, 1), (1, 2), (0, 2), (0, 3), (1, 3), (2, 0), (2, 1), (2, 2), (2, 3)):
             load_plane(g, t)
@@ -94,22 +94,28 @@ def tile_routed_moe_kernel(tc, xT, w, gate, offs, out):
         def slot_list(lo, hi):
             return offsets[:, lo // 16 : hi // 16]
 
+        def bf_view(g, lo, hi):
+            base = C if (g, C) in x_bf and lo >= C else 0
+            return x_bf[(g, base)][:, lo - base : hi - base, :]
+
         def scalar_gather(g, t, lo, hi):
-            nc.scalar.activation(x_bf[g][:, lo:hi, t], raw_bf[g][:, t, :].indirect(slot_list(lo, hi)), copy_fn)
+            nc.scalar.activation(
+                bf_view(g, lo, hi)[:, :, t], raw_bf[g][:, t, :].indirect(slot_list(lo, hi)), copy_fn
+            )
 
         def vector_gather(g, t):
-            nc.vector.tensor_copy(gathered[g][:, t, :], planes[(g, t)][:].indirect(offsets[:]))
-
-        def interleave(g, lo, hi):
-            nc.scalar.copy(x_bf[g][:, lo:hi, :], gathered[g][:, :, lo:hi].rearrange("p t c -> p c t"))
+            c0 = first_column(t)
+            nc.vector.tensor_copy(x_bf[(g, 0)][:, :, t], raw[g][:, c0 : c0 + WINDOW].indirect(offsets[:]))
 
         def quantize(g, lo, hi, codes, c0):
             nc.vector.quantize_mx(
                 out=codes[:, lo - c0 : hi - c0].bitcast(FP8X4),
                 scales=x_scales[g][:, lo:hi],
-                in_=x_bf[g][:, lo:hi, :].rearrange("p c t -> p (c t)"),
+                in_=bf_view(g, lo, hi).rearrange("p c t -> p (c t)"),
             )
-            x_codes[(g, lo)] = (codes, c0)
+            for i, (glo, ghi) in enumerate(GROUPS):
+                if lo <= glo and ghi <= hi:
+                    x_codes[(g, i)] = (codes, c0)
 
         def w_interleave(i):
             nc.vector.tensor_copy(
@@ -125,7 +131,7 @@ def tile_routed_moe_kernel(tc, xT, w, gate, offs, out):
 
         def multiply(g, i):
             lo, hi = GROUPS[i]
-            codes, c0 = x_codes[(g, lo)] if (g, lo) in x_codes else x_codes[(g, 0)]
+            codes, c0 = x_codes[(g, i)]
             col = ((g % 2) * E + lo // C) * N
             nc.tensor.matmul_mx(
                 out=acc[i][:],
@@ -148,10 +154,7 @@ def tile_routed_moe_kernel(tc, xT, w, gate, offs, out):
         for g in (FIRST_V, SECOND_V):
             for t in range(PACK):
                 vector_gather(g, t)
-        for g in (FIRST_V, SECOND_V):
-            for e in range(E):
-                interleave(g, e * C, (e + 1) * C)
-        nc.vector.tensor_copy(raw_bf[SECOND_S][:], raw[SECOND_S][:])
+        nc.scalar.copy(raw_bf[SECOND_S][:], raw[SECOND_S][:])
         for lo, hi in GROUPS:
             for t in range(PACK):
                 scalar_gather(SECOND_S, t, lo, hi)
@@ -160,27 +163,31 @@ def tile_routed_moe_kernel(tc, xT, w, gate, offs, out):
         codes_0 = held.tile([P, SLOTS], U32, name="codes_0", tag="raw_then_codes_0", align_bytes=64)
         quantize(0, 0, SLOTS, codes_0, 0)
         w_quantize(0)
+        w_interleave(1)
+        w_quantize(1)
         codes_1 = held.tile([P, SLOTS], U32, name="codes_1", tag="bf_then_codes_0", align_bytes=64)
         quantize(1, 0, SLOTS, codes_1, 0)
-        w_interleave(1)
-        codes_2 = held.tile([P, SLOTS], U32, name="codes_2", tag="raw_then_codes_1", align_bytes=64)
-        w_quantize(1)
-        quantize(2, 0, SLOTS, codes_2, 0)
+        codes_2a = held.tile([P, C], U32, name="codes_2a", tag="raw_then_codes_1", align_bytes=64)
+        quantize(2, 0, C, codes_2a, 0)
         codes_3 = held.tile([P, GROUPS[1][1]], U32, name="codes_3", tag="bf_then_codes_1", align_bytes=64)
+        quantize(3, 0, C, codes_3, 0)
+        for g in range(PASSES):
+            multiply(g, 0)
+        nc.vector.tensor_copy(sums[0][:], acc[0][:])
 
-        for i, (lo, hi) in enumerate(GROUPS):
-            if i == 2:
-                scatter(0)
-                codes_last = held.tile([P, hi - lo], U32, name="codes_last", tag="sums_0", align_bytes=64)
-                quantize(3, lo, hi, codes_last, lo)
-            else:
-                quantize(3, lo, hi, codes_3, 0)
-            for g in range(PASSES):
-                multiply(g, i)
-            if i == 0:
-                nc.vector.tensor_copy(sums[i][:], acc[i][:])
-            else:
-                nc.scalar.copy(sums[i][:], acc[i][:])
+        codes_2b = held.tile([P, C], U32, name="codes_2b", tag="bf_then_codes_2", align_bytes=64)
+        quantize(2, C, SLOTS, codes_2b, C)
+        quantize(3, GROUPS[1][0], GROUPS[1][1], codes_3, 0)
+        for g in range(PASSES):
+            multiply(g, 1)
+        nc.scalar.copy(sums[1][:], acc[1][:])
+
+        scatter(0)
+        codes_last = held.tile([P, GROUPS[2][1] - GROUPS[2][0]], U32, name="codes_last", tag="sums_0", align_bytes=64)
+        quantize(3, GROUPS[2][0], GROUPS[2][1], codes_last, GROUPS[2][0])
+        for g in range(PASSES):
+            multiply(g, 2)
+        nc.scalar.copy(sums[2][:], acc[2][:])
         scatter(1)
         scatter(2)
 

@@ -119,7 +119,8 @@ def tile_routed_moe_kernel(tc, xT, w, gate, offs, out):
 
         def w_interleave(i):
             nc.vector.tensor_copy(
-                w_bf[i][:].rearrange("p g e n j -> p (g e) n j"), w_raw[i][:].rearrange("p g e j n -> p (g e) n j")
+                w_bf[i][:].rearrange("p g e (c i) j -> p (g e) c j i", i=4),
+                w_raw[i][:].rearrange("p g e j (c i) -> p (g e) c j i", i=4),
             )
 
         def w_quantize(i):

@@ -49,7 +49,7 @@ def tile_routed_moe_kernel(tc, xT, w, gate, offs, out):
             raw[g] = held.tile([P, PACK, T], F32, name="raw_%d" % g)
             raw_bf[g] = held.tile([P, PACK, T], BF16, name="raw_bf_%d" % g)
         for g in (FIRST_V, SECOND_V):
-            raw[g] = held.tile([P, (PACK + 1) * T], F32, name="raw_%d" % g)
+            raw[g] = held.tile([P, (PACK + 1) * T], F32, name="raw_%d" % g, tag="raw_%d_then_codes" % g, align_bytes=64)
         for g in (FIRST_S, FIRST_V, SECOND_V):
             x_bf[(g, 0)] = held.tile([P, SLOTS, PACK], BF16, name="x_bf_%d" % g, align_bytes=64)
         x_bf[(SECOND_S, 0)] = held.tile([P, C, PACK], BF16, name="x_bf_3a", tag="bf_then_codes_2", align_bytes=64)
@@ -76,10 +76,22 @@ def tile_routed_moe_kernel(tc, xT, w, gate, offs, out):
             else:
                 nc.sync.dma_start(raw[g][:, first_column(t) : first_column(t) + T], x_planes[g, :, t, :])
 
-        for g, t in ((1, 0), (0, 0), (1, 1), (0, 1), (1, 2), (0, 2), (0, 3), (1, 3), (2, 0), (2, 1), (2, 2), (2, 3)):
-            load_plane(g, t)
-        nc.sync.dma_start(raw[SECOND_S][:], x_planes[SECOND_S])
-        for g in range(PASSES):
+        def load_w_block(g, e):
+            nc.sync.dma_start(w_raw[g // 2][:, g % 2, e], w_passes[g][:, e])
+
+        vector_planes = [(g, t) for g in (FIRST_V, SECOND_V) for t in range(PACK)]
+        scalar_planes = [(FIRST_S, t) for t in range(PACK)]
+        w_blocks = [(g, e) for g in range(2) for e in range(E)]
+        for kind in "VSVWVSWVSVWVSVWV":
+            if kind == "V":
+                load_plane(*vector_planes.pop(0))
+            elif kind == "S":
+                load_plane(*scalar_planes.pop(0))
+            else:
+                load_w_block(*w_blocks.pop(0))
+        for t in (0, 2):
+            nc.sync.dma_start(raw[SECOND_S][:, t : t + 2, :], x_planes[SECOND_S, :, t : t + 2, :])
+        for g in (2, 3):
             nc.sync.dma_start(w_raw[g // 2][:, g % 2], w_passes[g])
         nc.sync.dma_start(gate_sb[:], gate)
 
@@ -155,21 +167,24 @@ def tile_routed_moe_kernel(tc, xT, w, gate, offs, out):
         for g in (FIRST_V, SECOND_V):
             for t in range(PACK):
                 vector_gather(g, t)
-        nc.scalar.copy(raw_bf[SECOND_S][:], raw[SECOND_S][:])
+        for t in (0, 2):
+            nc.scalar.copy(raw_bf[SECOND_S][:, t : t + 2, :], raw[SECOND_S][:, t : t + 2, :])
         for lo, hi in GROUPS:
             for t in range(PACK):
                 scalar_gather(SECOND_S, t, lo, hi)
 
-        w_interleave(0)
-        codes_0 = held.tile([P, SLOTS], U32, name="codes_0", tag="raw_then_codes_0", align_bytes=64)
+        for g in range(2):
+            for e in range(E):
+                nc.gpsimd.tensor_copy(w_bf[0][:, g, e], w_raw[0][:, g, e].rearrange("p j n -> p n j"))
+        codes_1 = held.tile([P, SLOTS], U32, name="codes_1", tag="raw_2_then_codes", align_bytes=64)
+        quantize(1, 0, SLOTS, codes_1, 0)
+        codes_2a = held.tile([P, C], U32, name="codes_2a", align_bytes=64)
+        quantize(2, 0, C, codes_2a, 0)
+        codes_0 = held.tile([P, SLOTS], U32, name="codes_0", align_bytes=64)
         quantize(0, 0, SLOTS, codes_0, 0)
         w_quantize(0)
         w_interleave(1)
         w_quantize(1)
-        codes_1 = held.tile([P, SLOTS], U32, name="codes_1", tag="bf_then_codes_0", align_bytes=64)
-        quantize(1, 0, SLOTS, codes_1, 0)
-        codes_2a = held.tile([P, C], U32, name="codes_2a", tag="raw_then_codes_1", align_bytes=64)
-        quantize(2, 0, C, codes_2a, 0)
         codes_3 = held.tile([P, GROUPS[1][1]], U32, name="codes_3", tag="bf_then_codes_1", align_bytes=64)
         quantize(3, 0, C, codes_3, 0)
         for g in range(PASSES):

@@ -47,11 +47,14 @@ def tile_routed_moe_kernel(tc, xT, w, gate, offs, out):
         x_bf = {}
         for g in (FIRST_S, SECOND_S):
             raw[g] = held.tile([P, PACK, T], F32, name="raw_%d" % g)
-            raw_bf[g] = held.tile([P, PACK, T], BF16, name="raw_bf_%d" % g)
+        raw_bf[FIRST_S] = held.tile([P, (PACK + 1) * T], BF16, name="raw_bf_0")
+        raw_bf[SECOND_S] = held.tile([P, PACK, T], BF16, name="raw_bf_3")
         for g in (FIRST_V, SECOND_V):
             raw[g] = held.tile([P, (PACK + 1) * T], F32, name="raw_%d" % g, tag="raw_%d_then_codes" % g, align_bytes=64)
         for g in (FIRST_S, FIRST_V, SECOND_V):
-            x_bf[(g, 0)] = held.tile([P, SLOTS, PACK], BF16, name="x_bf_%d" % g, align_bytes=64)
+            x_bf[(g, 0)] = held.tile(
+                [P, SLOTS, PACK], BF16, name="x_bf_%d" % g, tag="x_bf_%d_then_codes" % g, align_bytes=64
+            )
         x_bf[(SECOND_S, 0)] = held.tile([P, C, PACK], BF16, name="x_bf_3a", tag="bf_then_codes_2", align_bytes=64)
         x_bf[(SECOND_S, C)] = held.tile([P, C, PACK], BF16, name="x_bf_3b", align_bytes=64)
         w_raw = [
@@ -161,9 +164,11 @@ def tile_routed_moe_kernel(tc, xT, w, gate, offs, out):
             nc.vector.tensor_tensor(result[:].indirect(slot_list(lo, hi)), sums[i][:], gate_sb[:, lo:hi], mult)
 
         for t in range(PACK):
-            nc.scalar.copy(raw_bf[FIRST_S][:, t, :], raw[FIRST_S][:, t, :])
-            for e in range(E):
-                scalar_gather(FIRST_S, t, e * C, (e + 1) * C)
+            c0 = first_column(t)
+            nc.scalar.copy(raw_bf[FIRST_S][:, c0 : c0 + T], raw[FIRST_S][:, t, :])
+            nc.scalar.activation(
+                x_bf[(FIRST_S, 0)][:, :, t], raw_bf[FIRST_S][:, c0 : c0 + WINDOW].indirect(offsets[:]), copy_fn
+            )
         for g in (FIRST_V, SECOND_V):
             for t in range(PACK):
                 vector_gather(g, t)
@@ -178,28 +183,27 @@ def tile_routed_moe_kernel(tc, xT, w, gate, offs, out):
                 nc.gpsimd.tensor_copy(w_bf[0][:, g, e], w_raw[0][:, g, e].rearrange("p j n -> p n j"))
         codes_1 = held.tile([P, SLOTS], U32, name="codes_1", tag="raw_2_then_codes", align_bytes=64)
         quantize(1, 0, SLOTS, codes_1, 0)
-        codes_2a = held.tile([P, C], U32, name="codes_2a", align_bytes=64)
-        quantize(2, 0, C, codes_2a, 0)
-        codes_0 = held.tile([P, SLOTS], U32, name="codes_0", align_bytes=64)
+        codes_2 = held.tile([P, SLOTS], U32, name="codes_2", align_bytes=64)
+        quantize(2, 0, SLOTS, codes_2, 0)
+        codes_0 = held.tile([P, SLOTS], U32, name="codes_0", tag="x_bf_1_then_codes", align_bytes=64)
         quantize(0, 0, SLOTS, codes_0, 0)
         w_quantize(0)
         w_interleave(1)
         w_quantize(1)
-        codes_3 = held.tile([P, GROUPS[1][1]], U32, name="codes_3", tag="bf_then_codes_1", align_bytes=64)
+        codes_3 = held.tile([P, C], U32, name="codes_3", tag="bf_then_codes_1", align_bytes=64)
         quantize(3, 0, C, codes_3, 0)
         for g in range(PASSES):
             multiply(g, 0)
         nc.vector.tensor_copy(sums[0][:], acc[0][:])
 
-        codes_2b = held.tile([P, C], U32, name="codes_2b", tag="bf_then_codes_2", align_bytes=64)
-        quantize(2, C, SLOTS, codes_2b, C)
-        quantize(3, GROUPS[1][0], GROUPS[1][1], codes_3, 0)
+        codes_3b = held.tile([P, C // 2], U32, name="codes_3b", tag="bf_then_codes_1", align_bytes=64)
+        quantize(3, GROUPS[1][0], GROUPS[1][1], codes_3b, GROUPS[1][0])
         for g in range(PASSES):
             multiply(g, 1)
         nc.scalar.copy(sums[1][:], acc[1][:])
 
         scatter(0)
-        codes_last = held.tile([P, GROUPS[2][1] - GROUPS[2][0]], U32, name="codes_last", tag="sums_0", align_bytes=64)
+        codes_last = held.tile([P, C // 2], U32, name="codes_last", tag="sums_0", align_bytes=64)
         quantize(3, GROUPS[2][0], GROUPS[2][1], codes_last, GROUPS[2][0])
         for g in range(PASSES):
             multiply(g, 2)

@@ -51,10 +51,9 @@ def tile_routed_moe_kernel(tc, xT, w, gate, offs, out):
         raw_bf[SECOND_S] = held.tile([P, PACK, T], BF16, name="raw_bf_3")
         for g in (FIRST_V, SECOND_V):
             raw[g] = held.tile([P, (PACK + 1) * T], F32, name="raw_%d" % g, tag="raw_%d_then_codes" % g, align_bytes=64)
-        for g in (FIRST_S, FIRST_V, SECOND_V):
-            x_bf[(g, 0)] = held.tile(
-                [P, SLOTS, PACK], BF16, name="x_bf_%d" % g, tag="x_bf_%d_then_codes" % g, align_bytes=64
-            )
+        gathered = {g: held.tile([P, PACK, SLOTS], F32, name="gathered_%d" % g) for g in (FIRST_V, SECOND_V)}
+        for g in (FIRST_S, SECOND_V):
+            x_bf[(g, 0)] = held.tile([P, SLOTS, PACK], BF16, name="x_bf_%d" % g, align_bytes=64)
         x_bf[(SECOND_S, 0)] = held.tile([P, C, PACK], BF16, name="x_bf_3a", tag="bf_then_codes_2", align_bytes=64)
         x_bf[(SECOND_S, C)] = held.tile([P, C, PACK], BF16, name="x_bf_3b", align_bytes=64)
         w_raw = [
@@ -85,7 +84,7 @@ def tile_routed_moe_kernel(tc, xT, w, gate, offs, out):
         vector_planes = [(g, t) for g in (FIRST_V, SECOND_V) for t in range(PACK)]
         scalar_planes = [(FIRST_S, t) for t in range(PACK)]
         w_blocks = [(g, e) for g in range(2) for e in range(E)]
-        for kind in "VSVWVSWVSVWVSVWV":
+        for kind in "VSVWVSWVSVWVSVV":
             if kind == "V":
                 load_plane(*vector_planes.pop(0))
             elif kind == "S":
@@ -94,6 +93,7 @@ def tile_routed_moe_kernel(tc, xT, w, gate, offs, out):
                 load_w_block(*w_blocks.pop(0))
         for t in (0, 2):
             nc.sync.dma_start(raw[SECOND_S][:, t : t + 2, :], x_planes[SECOND_S, :, t : t + 2, :])
+        load_w_block(*w_blocks.pop(0))
         for g in (2, 3):
             nc.sync.dma_start(w_raw[g // 2][:, g % 2], w_passes[g])
         nc.sync.dma_start(gate_sb[:], gate)
@@ -120,7 +120,13 @@ def tile_routed_moe_kernel(tc, xT, w, gate, offs, out):
 
         def vector_gather(g, t):
             c0 = first_column(t)
-            nc.vector.tensor_copy(x_bf[(g, 0)][:, :, t], raw[g][:, c0 : c0 + WINDOW].indirect(offsets[:]))
+            nc.vector.tensor_copy(gathered[g][:, t, :], raw[g][:, c0 : c0 + WINDOW].indirect(offsets[:]))
+
+        def x_interleave(g):
+            nc.vector.tensor_copy(
+                x_bf[(g, 0)][:].rearrange("p (c i) t -> p c t i", i=4),
+                gathered[g][:].rearrange("p t (c i) -> p c t i", i=4),
+            )
 
         def quantize(g, lo, hi, codes, c0):
             nc.vector.quantize_mx(
@@ -178,15 +184,21 @@ def tile_routed_moe_kernel(tc, xT, w, gate, offs, out):
             for t in range(PACK):
                 scalar_gather(SECOND_S, t, lo, hi)
 
-        for g in range(2):
-            for e in range(E):
-                nc.gpsimd.tensor_copy(w_bf[0][:, g, e], w_raw[0][:, g, e].rearrange("p j n -> p n j"))
-        codes_1 = held.tile([P, SLOTS], U32, name="codes_1", tag="raw_2_then_codes", align_bytes=64)
+        for g, e in ((0, 0), (0, 1), (1, 0)):
+            nc.gpsimd.tensor_copy(w_bf[0][:, g, e], w_raw[0][:, g, e].rearrange("p j n -> p n j"))
+        x_bf[(FIRST_V, 0)] = held.tile([P, SLOTS, PACK], BF16, name="x_bf_1", tag="raw_2_then_codes", align_bytes=64)
+        x_interleave(FIRST_V)
+        x_interleave(SECOND_V)
+        codes_1 = held.tile([P, SLOTS], U32, name="codes_1", align_bytes=64)
         quantize(1, 0, SLOTS, codes_1, 0)
         codes_2 = held.tile([P, SLOTS], U32, name="codes_2", align_bytes=64)
         quantize(2, 0, SLOTS, codes_2, 0)
-        codes_0 = held.tile([P, SLOTS], U32, name="codes_0", tag="x_bf_1_then_codes", align_bytes=64)
+        codes_0 = held.tile([P, SLOTS], U32, name="codes_0", tag="raw_2_then_codes", align_bytes=64)
         quantize(0, 0, SLOTS, codes_0, 0)
+        nc.vector.tensor_copy(
+            w_bf[0][:, 1, 1].rearrange("p (c i) j -> p c j i", i=4),
+            w_raw[0][:, 1, 1].rearrange("p j (c i) -> p c j i", i=4),
+        )
         w_quantize(0)
         w_interleave(1)
         w_quantize(1)

@@ -20,6 +20,7 @@ WINDOW = 2 * T
 
 FIRST_S, FIRST_V, SECOND_V, SECOND_S = 0, 1, 2, 3
 GROUPS = ((0, 256), (256, 384), (384, 512))
+GPSIMD_PASSES = 2
 
 
 def tile_routed_moe_kernel(tc, xT, w, gate, offs, out):
@@ -42,125 +43,79 @@ def tile_routed_moe_kernel(tc, xT, w, gate, offs, out):
         warm_out = held.tile([P, 1], F32, name="warm_out")
         nc.scalar.activation(warm_out[:], warm[:], copy_fn)
 
-        raw = {}
-        raw_bf = {}
-        x_bf = {}
-        for g in (FIRST_S, SECOND_S):
-            raw[g] = held.tile([P, PACK, T], F32, name="raw_%d" % g)
-        raw_bf[FIRST_S] = held.tile([P, (PACK + 1) * T], BF16, name="raw_bf_0")
-        raw_bf[SECOND_S] = held.tile([P, PACK, T], BF16, name="raw_bf_3")
-        for g in (FIRST_V, SECOND_V):
-            raw[g] = held.tile([P, (PACK + 1) * T], F32, name="raw_%d" % g, tag="raw_%d_then_codes" % g, align_bytes=64)
-        gathered = {g: held.tile([P, PACK, SLOTS], F32, name="gathered_%d" % g) for g in (FIRST_V, SECOND_V)}
-        for g in (FIRST_S, SECOND_V):
-            x_bf[(g, 0)] = held.tile([P, SLOTS, PACK], BF16, name="x_bf_%d" % g, align_bytes=64)
-        x_bf[(SECOND_S, 0)] = held.tile([P, C, PACK], BF16, name="x_bf_3a", tag="bf_then_codes_2", align_bytes=64)
-        x_bf[(SECOND_S, C)] = held.tile([P, C, PACK], BF16, name="x_bf_3b", align_bytes=64)
+        raw_v = {g: held.tile([P, (PACK + 1) * T], F32, name="raw_%d" % g) for g in (FIRST_V, SECOND_V)}
+        raw_s = {g: held.tile([P, PACK, T], F32, name="raw_%d" % g) for g in (FIRST_S, SECOND_S)}
+        bf_first = held.tile([P, (PACK + 1) * T], BF16, name="bf_first")
+        bf_last = held.tile([P, PACK, T], BF16, name="bf_last")
+        gathered = held.tile([P, 2, PACK, SLOTS], F32, name="gathered", tag="gathered_then_codes", align_bytes=64)
+        x_bf_v = held.tile([P, 2, SLOTS, PACK], BF16, name="x_bf_v", align_bytes=64)
+        x_bf_first = held.tile([P, SLOTS, PACK], BF16, name="x_bf_first", align_bytes=64)
+        x_bf_last = held.tile([P, SLOTS, PACK], BF16, name="x_bf_last", align_bytes=64)
         w_raw = [
-            held.tile([P, 2, E, PACK, N], F32, name="w_raw_%d" % i, tag="raw_then_codes_%d" % i, align_bytes=64)
-            for i in range(2)
+            held.tile([P, 2, E, PACK, N], F32, name="w_raw_%d" % h, tag="w_raw_%d_then_codes" % h, align_bytes=64)
+            for h in range(2)
         ]
         w_bf = [
-            held.tile([P, 2, E, N, PACK], BF16, name="w_bf_%d" % i, tag="bf_then_codes_%d" % i, align_bytes=64)
-            for i in range(2)
+            held.tile([P, 2, E, N, PACK], BF16, name="w_bf_%d" % h, tag="w_bf_%d_then_codes" % h, align_bytes=64)
+            for h in range(2)
         ]
-        w_codes = [held.tile([P, 2 * E * N], U32, name="w_codes_%d" % i, align_bytes=64) for i in range(2)]
-        w_scales = [held.tile([P, 2 * E * N], U8, name="w_scales_%d" % i, align_bytes=64) for i in range(2)]
+        w_codes = held.tile([P, PASSES * E * N], U32, name="w_codes", align_bytes=64)
+        w_scales = held.tile([P, PASSES * E * N], U8, name="w_scales", align_bytes=64)
+        scales_v = held.tile([P, 2 * SLOTS], U8, name="scales_v", align_bytes=64)
+        scales_first = held.tile([P, SLOTS], U8, name="scales_first", align_bytes=64)
+        scales_last = held.tile([P, SLOTS], U8, name="scales_last", align_bytes=64)
         gate_sb = held.tile([P, SLOTS], F32, name="gate_sb")
         result = held.tile([N, T], F32, name="result")
-
-        def first_column(t):
-            return (PACK - 1 - t) * T
-
-        def load_plane(g, t):
-            if g in raw_bf:
-                nc.sync.dma_start(raw[g][:, t, :], x_planes[g, :, t, :])
-            else:
-                nc.sync.dma_start(raw[g][:, first_column(t) : first_column(t) + T], x_planes[g, :, t, :])
-
-        def load_w_block(g, e):
-            nc.sync.dma_start(w_raw[g // 2][:, g % 2, e], w_passes[g][:, e])
-
-        vector_planes = [(g, t) for g in (FIRST_V, SECOND_V) for t in range(PACK)]
-        scalar_planes = [(FIRST_S, t) for t in range(PACK)]
-        w_blocks = [(g, e) for g in range(2) for e in range(E)]
-        for kind in "VSVWVSWVSVWVSVV":
-            if kind == "V":
-                load_plane(*vector_planes.pop(0))
-            elif kind == "S":
-                load_plane(*scalar_planes.pop(0))
-            else:
-                load_w_block(*w_blocks.pop(0))
-        for t in (0, 2):
-            nc.sync.dma_start(raw[SECOND_S][:, t : t + 2, :], x_planes[SECOND_S, :, t : t + 2, :])
-        load_w_block(*w_blocks.pop(0))
-        for g in (2, 3):
-            nc.sync.dma_start(w_raw[g // 2][:, g % 2], w_passes[g])
-        nc.sync.dma_start(gate_sb[:], gate)
-
         acc = [psum.tile([N, hi - lo], F32, name="acc_%d" % i) for i, (lo, hi) in enumerate(GROUPS)]
         sums = [
             held.tile([N, hi - lo], F32, name="sums_%d" % i, tag="sums_%d" % i, align_bytes=64)
             for i, (lo, hi) in enumerate(GROUPS)
         ]
-        x_scales = [held.tile([P, SLOTS], U8, name="x_scales_%d" % g, align_bytes=64) for g in range(PASSES)]
-        x_codes = {}
+
+        def first_column(t):
+            return (PACK - 1 - t) * T
+
+        def load_plane(g, t):
+            if g in raw_s:
+                nc.sync.dma_start(raw_s[g][:, t, :], x_planes[g, :, t, :])
+            else:
+                nc.sync.dma_start(raw_v[g][:, first_column(t) : first_column(t) + T], x_planes[g, :, t, :])
+
+        vector_planes = [(g, t) for g in (FIRST_V, SECOND_V) for t in range(PACK)]
+        scalar_planes = [(FIRST_S, t) for t in range(PACK)]
+        w_blocks = [(g, e) for g in range(GPSIMD_PASSES) for e in range(E)]
+        for kind in "VSVWVSWVSVWVSVWV":
+            if kind == "V":
+                load_plane(*vector_planes.pop(0))
+            elif kind == "S":
+                load_plane(*scalar_planes.pop(0))
+            else:
+                g, e = w_blocks.pop(0)
+                nc.sync.dma_start(w_raw[0][:, g, e], w_passes[g][:, e])
+        for t in (0, 2):
+            nc.sync.dma_start(raw_s[SECOND_S][:, t : t + 2, :], x_planes[SECOND_S, :, t : t + 2, :])
+        for g in range(GPSIMD_PASSES, PASSES):
+            nc.sync.dma_start(w_raw[1][:, g - GPSIMD_PASSES], w_passes[g])
+        nc.sync.dma_start(gate_sb[:], gate)
 
         def slot_list(lo, hi):
             return offsets[:, lo // 16 : hi // 16]
 
-        def bf_view(g, lo, hi):
-            base = C if (g, C) in x_bf and lo >= C else 0
-            return x_bf[(g, base)][:, lo - base : hi - base, :]
+        def quantize(x_bf, codes, scales):
+            nc.vector.quantize_mx(out=codes.bitcast(FP8X4), scales=scales, in_=x_bf)
 
-        def scalar_gather(g, t, lo, hi):
-            nc.scalar.activation(
-                bf_view(g, lo, hi)[:, :, t], raw_bf[g][:, t, :].indirect(slot_list(lo, hi)), copy_fn
-            )
-
-        def vector_gather(g, t):
-            c0 = first_column(t)
-            nc.vector.tensor_copy(gathered[g][:, t, :], raw[g][:, c0 : c0 + WINDOW].indirect(offsets[:]))
-
-        def x_interleave(g):
-            nc.vector.tensor_copy(
-                x_bf[(g, 0)][:].rearrange("p (c i) t -> p c t i", i=4),
-                gathered[g][:].rearrange("p t (c i) -> p c t i", i=4),
-            )
-
-        def quantize(g, lo, hi, codes, c0):
-            nc.vector.quantize_mx(
-                out=codes[:, lo - c0 : hi - c0].bitcast(FP8X4),
-                scales=x_scales[g][:, lo:hi],
-                in_=bf_view(g, lo, hi).rearrange("p c t -> p (c t)"),
-            )
-            for i, (glo, ghi) in enumerate(GROUPS):
-                if lo <= glo and ghi <= hi:
-                    x_codes[(g, i)] = (codes, c0)
-
-        def w_interleave(i):
-            nc.vector.tensor_copy(
-                w_bf[i][:].rearrange("p g e (c i) j -> p (g e) c j i", i=4),
-                w_raw[i][:].rearrange("p g e j (c i) -> p (g e) c j i", i=4),
-            )
-
-        def w_quantize(i):
-            nc.vector.quantize_mx(
-                out=w_codes[i][:].bitcast(FP8X4),
-                scales=w_scales[i][:],
-                in_=w_bf[i][:].rearrange("p g e n j -> p (g e n j)"),
-            )
+        x_operands = {}
 
         def multiply(g, i):
             lo, hi = GROUPS[i]
-            codes, c0 = x_codes[(g, i)]
-            col = ((g % 2) * E + lo // C) * N
+            codes, scales = x_operands[(g, i)]
+            col = (g * E + lo // C) * N
             nc.tensor.matmul_mx(
                 out=acc[i][:],
-                lhsT=w_codes[g // 2][:, col : col + N].bitcast(FP8X4),
-                lhsT_scale=w_scales[g // 2][:, col : col + N],
-                rhs=codes[:, lo - c0 : hi - c0].bitcast(FP8X4),
-                rhs_scale=x_scales[g][:, lo:hi],
+                lhsT=w_codes[:, col : col + N].bitcast(FP8X4),
+                lhsT_scale=w_scales[:, col : col + N],
+                rhs=codes.bitcast(FP8X4),
+                rhs_scale=scales,
                 start=(g == 0),
                 stop=(g == PASSES - 1),
             )
@@ -171,54 +126,63 @@ def tile_routed_moe_kernel(tc, xT, w, gate, offs, out):
 
         for t in range(PACK):
             c0 = first_column(t)
-            nc.scalar.copy(raw_bf[FIRST_S][:, c0 : c0 + T], raw[FIRST_S][:, t, :])
-            nc.scalar.activation(
-                x_bf[(FIRST_S, 0)][:, :, t], raw_bf[FIRST_S][:, c0 : c0 + WINDOW].indirect(offsets[:]), copy_fn
-            )
-        for g in (FIRST_V, SECOND_V):
+            nc.scalar.copy(bf_first[:, c0 : c0 + T], raw_s[FIRST_S][:, t, :])
+            nc.scalar.activation(x_bf_first[:, :, t], bf_first[:, c0 : c0 + WINDOW].indirect(offsets[:]), copy_fn)
+        for u, g in enumerate((FIRST_V, SECOND_V)):
             for t in range(PACK):
-                vector_gather(g, t)
+                c0 = first_column(t)
+                nc.vector.tensor_copy(gathered[:, u, t, :], raw_v[g][:, c0 : c0 + WINDOW].indirect(offsets[:]))
         for t in (0, 2):
-            nc.scalar.copy(raw_bf[SECOND_S][:, t : t + 2, :], raw[SECOND_S][:, t : t + 2, :])
+            nc.scalar.copy(bf_last[:, t : t + 2, :], raw_s[SECOND_S][:, t : t + 2, :])
         for lo, hi in GROUPS:
             for t in range(PACK):
-                scalar_gather(SECOND_S, t, lo, hi)
+                nc.scalar.activation(x_bf_last[:, lo:hi, t], bf_last[:, t, :].indirect(slot_list(lo, hi)), copy_fn)
+        for g in range(GPSIMD_PASSES):
+            for e in range(E):
+                nc.gpsimd.tensor_copy(w_bf[0][:, g, e], w_raw[0][:, g, e].rearrange("p j n -> p n j"))
 
-        for g, e in ((0, 0), (0, 1), (1, 0)):
-            nc.gpsimd.tensor_copy(w_bf[0][:, g, e], w_raw[0][:, g, e].rearrange("p j n -> p n j"))
-        x_bf[(FIRST_V, 0)] = held.tile([P, SLOTS, PACK], BF16, name="x_bf_1", tag="raw_2_then_codes", align_bytes=64)
-        x_interleave(FIRST_V)
-        x_interleave(SECOND_V)
-        codes_1 = held.tile([P, SLOTS], U32, name="codes_1", align_bytes=64)
-        quantize(1, 0, SLOTS, codes_1, 0)
-        codes_2 = held.tile([P, SLOTS], U32, name="codes_2", align_bytes=64)
-        quantize(2, 0, SLOTS, codes_2, 0)
-        codes_0 = held.tile([P, SLOTS], U32, name="codes_0", tag="raw_2_then_codes", align_bytes=64)
-        quantize(0, 0, SLOTS, codes_0, 0)
         nc.vector.tensor_copy(
-            w_bf[0][:, 1, 1].rearrange("p (c i) j -> p c j i", i=4),
-            w_raw[0][:, 1, 1].rearrange("p j (c i) -> p c j i", i=4),
+            x_bf_v[:].rearrange("p u (c i) t -> p u c t i", i=4), gathered[:].rearrange("p u t (c i) -> p u c t i", i=4)
         )
+        half = 2 * E * N
+
+        def w_quantize(h):
+            quantize(
+                w_bf[h][:].rearrange("p g e n j -> p (g e n j)"),
+                w_codes[:, h * half : (h + 1) * half],
+                w_scales[:, h * half : (h + 1) * half],
+            )
+
         w_quantize(0)
-        w_interleave(1)
+        codes_first = held.tile([P, SLOTS], U32, name="codes_first", tag="gathered_then_codes", align_bytes=64)
+        quantize(x_bf_first[:].rearrange("p c t -> p (c t)"), codes_first[:], scales_first[:])
+        nc.vector.tensor_copy(
+            w_bf[1][:].rearrange("p g e (c i) j -> p (g e) c j i", i=4),
+            w_raw[1][:].rearrange("p g e j (c i) -> p (g e) c j i", i=4),
+        )
+        codes_v = held.tile([P, 2 * SLOTS], U32, name="codes_v", tag="w_raw_1_then_codes", align_bytes=64)
+        quantize(x_bf_v[:].rearrange("p u c t -> p (u c t)"), codes_v[:], scales_v[:])
         w_quantize(1)
-        codes_3 = held.tile([P, C], U32, name="codes_3", tag="bf_then_codes_1", align_bytes=64)
-        quantize(3, 0, C, codes_3, 0)
-        for g in range(PASSES):
-            multiply(g, 0)
+        for i, (lo, hi) in enumerate(GROUPS):
+            x_operands[(FIRST_S, i)] = (codes_first[:, lo:hi], scales_first[:, lo:hi])
+            for u, g in enumerate((FIRST_V, SECOND_V)):
+                x_operands[(g, i)] = (codes_v[:, u * SLOTS + lo : u * SLOTS + hi], scales_v[:, u * SLOTS + lo : u * SLOTS + hi])
+
+        def quantize_last(i, codes):
+            lo, hi = GROUPS[i]
+            quantize(x_bf_last[:, lo:hi, :].rearrange("p c t -> p (c t)"), codes, scales_last[:, lo:hi])
+            x_operands[(SECOND_S, i)] = (codes, scales_last[:, lo:hi])
+            for g in range(PASSES):
+                multiply(g, i)
+
+        codes_last_01 = held.tile([P, GROUPS[1][1]], U32, name="codes_last_01", tag="w_bf_1_then_codes", align_bytes=64)
+        quantize_last(0, codes_last_01[:, GROUPS[0][0] : GROUPS[0][1]])
+        quantize_last(1, codes_last_01[:, GROUPS[1][0] : GROUPS[1][1]])
         nc.vector.tensor_copy(sums[0][:], acc[0][:])
-
-        codes_3b = held.tile([P, C // 2], U32, name="codes_3b", tag="bf_then_codes_1", align_bytes=64)
-        quantize(3, GROUPS[1][0], GROUPS[1][1], codes_3b, GROUPS[1][0])
-        for g in range(PASSES):
-            multiply(g, 1)
         nc.scalar.copy(sums[1][:], acc[1][:])
-
         scatter(0)
-        codes_last = held.tile([P, C // 2], U32, name="codes_last", tag="sums_0", align_bytes=64)
-        quantize(3, GROUPS[2][0], GROUPS[2][1], codes_last, GROUPS[2][0])
-        for g in range(PASSES):
-            multiply(g, 2)
+        codes_last_2 = held.tile([P, C // 2], U32, name="codes_last_2", tag="sums_0", align_bytes=64)
+        quantize_last(2, codes_last_2[:])
         nc.scalar.copy(sums[2][:], acc[2][:])
         scatter(1)
         scatter(2)

@@ -141,8 +141,9 @@ def tile_routed_moe_kernel(tc, xT, w, gate, offs, out):
             for e in range(E):
                 nc.gpsimd.tensor_copy(w_bf[0][:, g, e], w_raw[0][:, g, e].rearrange("p j n -> p n j"))
 
+        nc.gpsimd.tensor_copy(x_bf_v[:, 0], gathered[:, 0].rearrange("p t c -> p c t"))
         nc.vector.tensor_copy(
-            x_bf_v[:].rearrange("p u (c i) t -> p u c t i", i=4), gathered[:].rearrange("p u t (c i) -> p u c t i", i=4)
+            x_bf_v[:, 1].rearrange("p (c i) t -> p c t i", i=4), gathered[:, 1].rearrange("p t (c i) -> p c t i", i=4)
         )
         half = 2 * E * N
 

@@ -36,7 +36,6 @@ def tile_routed_moe_kernel(tc, xT, w, gate, offs, out):
         psum = ctx.enter_context(tc.psum_pool(name="psum", bufs=1))
 
         offsets = lists.tile([P, SLOTS // 16], U16, name="offsets")
-        nc.sync.dma_start(offsets[:], offs)
 
         warm = held.tile([P, 1], F32, name="warm")
         nc.vector.memset(warm[:], 0.0)
@@ -84,8 +83,10 @@ def tile_routed_moe_kernel(tc, xT, w, gate, offs, out):
         vector_planes = [(g, t) for g in (FIRST_V, SECOND_V) for t in range(PACK)]
         scalar_planes = [(FIRST_S, t) for t in range(PACK)]
         w_blocks = [(g, e) for g in range(GPSIMD_PASSES) for e in range(E)]
-        for kind in "VSVWVSWVSVWVSVWV":
-            if kind == "V":
+        for kind in "VOSVWVSWVSVWVSVWV":
+            if kind == "O":
+                nc.sync.dma_start(offsets[:], offs)
+            elif kind == "V":
                 load_plane(*vector_planes.pop(0))
             elif kind == "S":
                 load_plane(*scalar_planes.pop(0))
@@ -176,10 +177,11 @@ def tile_routed_moe_kernel(tc, xT, w, gate, offs, out):
             for g in range(PASSES):
                 multiply(g, i)
 
-        codes_last_01 = held.tile([P, GROUPS[1][1]], U32, name="codes_last_01", tag="w_bf_1_then_codes", align_bytes=64)
-        quantize_last(0, codes_last_01[:, GROUPS[0][0] : GROUPS[0][1]])
-        quantize_last(1, codes_last_01[:, GROUPS[1][0] : GROUPS[1][1]])
+        codes_last_0 = held.tile([P, C], U32, name="codes_last_0", tag="w_bf_1_then_codes", align_bytes=64)
+        quantize_last(0, codes_last_0[:])
         nc.vector.tensor_copy(sums[0][:], acc[0][:])
+        codes_last_1 = held.tile([P, C // 2], U32, name="codes_last_1", tag="w_bf_1_then_codes", align_bytes=64)
+        quantize_last(1, codes_last_1[:])
         nc.scalar.copy(sums[1][:], acc[1][:])
         scatter(0)
         codes_last_2 = held.tile([P, C // 2], U32, name="codes_last_2", tag="sums_0", align_bytes=64)

@@ -20,7 +20,8 @@ WINDOW = 2 * T
 
 FIRST_S, FIRST_V, SECOND_V, SECOND_S = 0, 1, 2, 3
 GROUPS = ((0, 256), (256, 384), (384, 512))
-GPSIMD_PASSES = 2
+GPSIMD_PASSES = 1
+GPSIMD_PLANE = 2
 
 
 def tile_routed_moe_kernel(tc, xT, w, gate, offs, out):
@@ -50,10 +51,9 @@ def tile_routed_moe_kernel(tc, xT, w, gate, offs, out):
         x_bf_v = held.tile([P, 2, SLOTS, PACK], BF16, name="x_bf_v", align_bytes=64)
         x_bf_first = held.tile([P, SLOTS, PACK], BF16, name="x_bf_first", align_bytes=64)
         x_bf_last = held.tile([P, SLOTS, PACK], BF16, name="x_bf_last", align_bytes=64)
-        w_raw = [
-            held.tile([P, 2, E, PACK, N], F32, name="w_raw_%d" % h, tag="w_raw_%d_then_codes" % h, align_bytes=64)
-            for h in range(2)
-        ]
+        w_raw_0 = held.tile([P, E, PACK, N], F32, name="w_raw_0")
+        w_raw_1 = held.tile([P, E, PACK, N], F32, name="w_raw_1", tag="w_raw_1_then_codes", align_bytes=64)
+        w_raw_23 = held.tile([P, E, 2, PACK, N], F32, name="w_raw_23", tag="w_raw_23_then_codes", align_bytes=64)
         w_bf = [
             held.tile([P, 2, E, N, PACK], BF16, name="w_bf_%d" % h, tag="w_bf_%d_then_codes" % h, align_bytes=64)
             for h in range(2)
@@ -81,9 +81,9 @@ def tile_routed_moe_kernel(tc, xT, w, gate, offs, out):
                 nc.sync.dma_start(raw_v[g][:, first_column(t) : first_column(t) + T], x_planes[g, :, t, :])
 
         vector_planes = [(g, t) for g in (FIRST_V, SECOND_V) for t in range(PACK)]
-        scalar_planes = [(FIRST_S, t) for t in range(PACK)]
+        scalar_planes = [(FIRST_S, t) for t in range(PACK)] + [(SECOND_S, 0), (SECOND_S, 1)]
         w_blocks = [(g, e) for g in range(GPSIMD_PASSES) for e in range(E)]
-        for kind in "VOSVWVSWVSVWVSVWV":
+        for kind in "VOSVSVSVWVWVSVSVS":
             if kind == "O":
                 nc.sync.dma_start(offsets[:], offs)
             elif kind == "V":
@@ -92,11 +92,11 @@ def tile_routed_moe_kernel(tc, xT, w, gate, offs, out):
                 load_plane(*scalar_planes.pop(0))
             else:
                 g, e = w_blocks.pop(0)
-                nc.sync.dma_start(w_raw[0][:, g, e], w_passes[g][:, e])
-        for t in (0, 2):
-            nc.sync.dma_start(raw_s[SECOND_S][:, t : t + 2, :], x_planes[SECOND_S, :, t : t + 2, :])
-        for g in range(GPSIMD_PASSES, PASSES):
-            nc.sync.dma_start(w_raw[1][:, g - GPSIMD_PASSES], w_passes[g])
+                nc.sync.dma_start(w_raw_0[:, e], w_passes[g][:, e])
+        nc.sync.dma_start(raw_s[SECOND_S][:, 2:4, :], x_planes[SECOND_S, :, 2:4, :])
+        nc.sync.dma_start(w_raw_1[:], w_passes[1])
+        for g in (2, 3):
+            nc.sync.dma_start(w_raw_23[:, :, g - 2], w_passes[g])
         nc.sync.dma_start(gate_sb[:], gate)
 
         def slot_list(lo, hi):
@@ -110,7 +110,8 @@ def tile_routed_moe_kernel(tc, xT, w, gate, offs, out):
         def multiply(g, i):
             lo, hi = GROUPS[i]
             codes, scales = x_operands[(g, i)]
-            col = (g * E + lo // C) * N
+            e = lo // C
+            col = (g * E + e) * N if g < 2 else (2 * E + e * 2 + g - 2) * N
             nc.tensor.matmul_mx(
                 out=acc[i][:],
                 lhsT=w_codes[:, col : col + N].bitcast(FP8X4),
@@ -127,7 +128,10 @@ def tile_routed_moe_kernel(tc, xT, w, gate, offs, out):
 
         for t in range(PACK):
             c0 = first_column(t)
-            nc.scalar.copy(bf_first[:, c0 : c0 + T], raw_s[FIRST_S][:, t, :])
+            if t == GPSIMD_PLANE:
+                nc.gpsimd.tensor_copy(bf_first[:, c0 : c0 + T], raw_s[FIRST_S][:, t, :])
+            else:
+                nc.scalar.copy(bf_first[:, c0 : c0 + T], raw_s[FIRST_S][:, t, :])
             nc.scalar.activation(x_bf_first[:, :, t], bf_first[:, c0 : c0 + WINDOW].indirect(offsets[:]), copy_fn)
         for u, g in enumerate((FIRST_V, SECOND_V)):
             for t in range(PACK):
@@ -140,7 +144,7 @@ def tile_routed_moe_kernel(tc, xT, w, gate, offs, out):
                 nc.scalar.activation(x_bf_last[:, lo:hi, t], bf_last[:, t, :].indirect(slot_list(lo, hi)), copy_fn)
         for g in range(GPSIMD_PASSES):
             for e in range(E):
-                nc.gpsimd.tensor_copy(w_bf[0][:, g, e], w_raw[0][:, g, e].rearrange("p j n -> p n j"))
+                nc.gpsimd.tensor_copy(w_bf[0][:, g, e], w_raw_0[:, e].rearrange("p j n -> p n j"))
 
         nc.gpsimd.tensor_copy(x_bf_v[:, 0], gathered[:, 0].rearrange("p t c -> p c t"))
         nc.vector.tensor_copy(
@@ -148,23 +152,23 @@ def tile_routed_moe_kernel(tc, xT, w, gate, offs, out):
         )
         half = 2 * E * N
 
-        def w_quantize(h):
-            quantize(
-                w_bf[h][:].rearrange("p g e n j -> p (g e n j)"),
-                w_codes[:, h * half : (h + 1) * half],
-                w_scales[:, h * half : (h + 1) * half],
-            )
 
-        w_quantize(0)
+        def w_quantize_expert(e):
+            cols = slice(half + e * 2 * N, half + (e + 1) * 2 * N)
+            quantize(w_bf[1][:, e].rearrange("p g n j -> p (g n j)"), w_codes[:, cols], w_scales[:, cols])
+
         codes_first = held.tile([P, SLOTS], U32, name="codes_first", tag="gathered_then_codes", align_bytes=64)
         quantize(x_bf_first[:].rearrange("p c t -> p (c t)"), codes_first[:], scales_first[:])
         nc.vector.tensor_copy(
-            w_bf[1][:].rearrange("p g e (c i) j -> p (g e) c j i", i=4),
-            w_raw[1][:].rearrange("p g e j (c i) -> p (g e) c j i", i=4),
+            w_bf[0][:, 1].rearrange("p e (c i) j -> p e c j i", i=4), w_raw_1[:].rearrange("p e j (c i) -> p e c j i", i=4)
         )
         codes_v = held.tile([P, 2 * SLOTS], U32, name="codes_v", tag="w_raw_1_then_codes", align_bytes=64)
         quantize(x_bf_v[:].rearrange("p u c t -> p (u c t)"), codes_v[:], scales_v[:])
-        w_quantize(1)
+        quantize(w_bf[0][:].rearrange("p g e n j -> p (g e n j)"), w_codes[:, 0:half], w_scales[:, 0:half])
+        nc.vector.tensor_copy(
+            w_bf[1][:].rearrange("p e g (c i) j -> p (e g) c j i", i=4),
+            w_raw_23[:].rearrange("p e g j (c i) -> p (e g) c j i", i=4),
+        )
         for i, (lo, hi) in enumerate(GROUPS):
             x_operands[(FIRST_S, i)] = (codes_first[:, lo:hi], scales_first[:, lo:hi])
             for u, g in enumerate((FIRST_V, SECOND_V)):
@@ -177,10 +181,16 @@ def tile_routed_moe_kernel(tc, xT, w, gate, offs, out):
             for g in range(PASSES):
                 multiply(g, i)
 
-        codes_last_0 = held.tile([P, C], U32, name="codes_last_0", tag="w_bf_1_then_codes", align_bytes=64)
-        quantize_last(0, codes_last_0[:])
+        codes_last_0 = held.tile([P, C], U32, name="codes_last_0", tag="w_raw_23_then_codes", align_bytes=64)
+        lo, hi = GROUPS[0]
+        quantize(x_bf_last[:, lo:hi, :].rearrange("p c t -> p (c t)"), codes_last_0[:], scales_last[:, lo:hi])
+        x_operands[(SECOND_S, 0)] = (codes_last_0[:], scales_last[:, lo:hi])
+        w_quantize_expert(0)
+        for g in range(PASSES):
+            multiply(g, 0)
+        w_quantize_expert(1)
         nc.vector.tensor_copy(sums[0][:], acc[0][:])
-        codes_last_1 = held.tile([P, C // 2], U32, name="codes_last_1", tag="w_bf_1_then_codes", align_bytes=64)
+        codes_last_1 = held.tile([P, C // 2], U32, name="codes_last_1", tag="w_raw_23_then_codes", align_bytes=64)
         quantize_last(1, codes_last_1[:])
         nc.scalar.copy(sums[1][:], acc[1][:])
         scatter(0)

@@ -45,14 +45,17 @@ def tile_routed_moe_kernel(tc, xT, w, gate, offs, out):
 
         raw_v = {g: held.tile([P, (PACK + 1) * T], F32, name="raw_%d" % g) for g in (FIRST_V, SECOND_V)}
         raw_s = {g: held.tile([P, PACK, T], F32, name="raw_%d" % g) for g in (FIRST_S, SECOND_S)}
+        raw_for_gpsimd = held.tile([P, T], F32, name="raw_for_gpsimd", tag="raw_then_x_bf_v", align_bytes=64)
         bf_first = held.tile([P, (PACK + 1) * T], BF16, name="bf_first")
         bf_last = held.tile([P, PACK, T], BF16, name="bf_last")
         gathered = held.tile([P, 2, PACK, SLOTS], F32, name="gathered", tag="gathered_then_codes", align_bytes=64)
-        x_bf_v = held.tile([P, 2, SLOTS, PACK], BF16, name="x_bf_v", align_bytes=64)
         x_bf_first = held.tile([P, SLOTS, PACK], BF16, name="x_bf_first", align_bytes=64)
         x_bf_last = held.tile([P, SLOTS, PACK], BF16, name="x_bf_last", align_bytes=64)
         w_raw_0 = held.tile([P, E, PACK, N], F32, name="w_raw_0")
-        w_raw_1 = held.tile([P, E, PACK, N], F32, name="w_raw_1", tag="w_raw_1_then_codes", align_bytes=64)
+        w_raw_1 = [
+            held.tile([P, PACK, N], F32, name="w_raw_1_%d" % e, tag="w_raw_1_%d_then_codes" % e, align_bytes=64)
+            for e in range(E)
+        ]
         w_raw_23 = held.tile([P, E, 2, PACK, N], F32, name="w_raw_23", tag="w_raw_23_then_codes", align_bytes=64)
         w_bf = [
             held.tile([P, 2, E, N, PACK], BF16, name="w_bf_%d" % h, tag="w_bf_%d_then_codes" % h, align_bytes=64)
@@ -75,15 +78,17 @@ def tile_routed_moe_kernel(tc, xT, w, gate, offs, out):
             return (PACK - 1 - t) * T
 
         def load_plane(g, t):
-            if g in raw_s:
+            if (g, t) == (FIRST_S, GPSIMD_PLANE):
+                nc.sync.dma_start(raw_for_gpsimd[:], x_planes[g, :, t, :])
+            elif g in raw_s:
                 nc.sync.dma_start(raw_s[g][:, t, :], x_planes[g, :, t, :])
             else:
                 nc.sync.dma_start(raw_v[g][:, first_column(t) : first_column(t) + T], x_planes[g, :, t, :])
 
         vector_planes = [(g, t) for g in (FIRST_V, SECOND_V) for t in range(PACK)]
         scalar_planes = [(FIRST_S, t) for t in range(PACK)] + [(SECOND_S, 0), (SECOND_S, 1)]
-        w_blocks = [(g, e) for g in range(GPSIMD_PASSES) for e in range(E)]
-        for kind in "VOSVSVSVWVWVSVSVS":
+        w_blocks = [(0, 0), (0, 1), (1, 0), (1, 1)]
+        for kind in "VOSVWVSVSWVVSVWVWSS":
             if kind == "O":
                 nc.sync.dma_start(offsets[:], offs)
             elif kind == "V":
@@ -92,9 +97,8 @@ def tile_routed_moe_kernel(tc, xT, w, gate, offs, out):
                 load_plane(*scalar_planes.pop(0))
             else:
                 g, e = w_blocks.pop(0)
-                nc.sync.dma_start(w_raw_0[:, e], w_passes[g][:, e])
+                nc.sync.dma_start(w_raw_0[:, e] if g == 0 else w_raw_1[e][:], w_passes[g][:, e])
         nc.sync.dma_start(raw_s[SECOND_S][:, 2:4, :], x_planes[SECOND_S, :, 2:4, :])
-        nc.sync.dma_start(w_raw_1[:], w_passes[1])
         for g in (2, 3):
             nc.sync.dma_start(w_raw_23[:, :, g - 2], w_passes[g])
         nc.sync.dma_start(gate_sb[:], gate)
@@ -129,7 +133,7 @@ def tile_routed_moe_kernel(tc, xT, w, gate, offs, out):
         for t in range(PACK):
             c0 = first_column(t)
             if t == GPSIMD_PLANE:
-                nc.gpsimd.tensor_copy(bf_first[:, c0 : c0 + T], raw_s[FIRST_S][:, t, :])
+                nc.gpsimd.tensor_copy(bf_first[:, c0 : c0 + T], raw_for_gpsimd[:])
             else:
                 nc.scalar.copy(bf_first[:, c0 : c0 + T], raw_s[FIRST_S][:, t, :])
             nc.scalar.activation(x_bf_first[:, :, t], bf_first[:, c0 : c0 + WINDOW].indirect(offsets[:]), copy_fn)
@@ -142,11 +146,13 @@ def tile_routed_moe_kernel(tc, xT, w, gate, offs, out):
         for lo, hi in GROUPS:
             for t in range(PACK):
                 nc.scalar.activation(x_bf_last[:, lo:hi, t], bf_last[:, t, :].indirect(slot_list(lo, hi)), copy_fn)
-        for g in range(GPSIMD_PASSES):
-            for e in range(E):
-                nc.gpsimd.tensor_copy(w_bf[0][:, g, e], w_raw_0[:, e].rearrange("p j n -> p n j"))
+        for e in range(E):
+            nc.gpsimd.tensor_copy(w_bf[0][:, 0, e], w_raw_0[:, e].rearrange("p j n -> p n j"))
 
+        x_bf_v = held.tile([P, 2, SLOTS, PACK], BF16, name="x_bf_v", tag="raw_then_x_bf_v", align_bytes=64)
         nc.gpsimd.tensor_copy(x_bf_v[:, 0], gathered[:, 0].rearrange("p t c -> p c t"))
+        for e in range(E):
+            nc.gpsimd.tensor_copy(w_bf[0][:, 1, e], w_raw_1[e][:].rearrange("p j n -> p n j"))
         nc.vector.tensor_copy(
             x_bf_v[:, 1].rearrange("p (c i) t -> p c t i", i=4), gathered[:, 1].rearrange("p t (c i) -> p c t i", i=4)
         )
@@ -159,10 +165,7 @@ def tile_routed_moe_kernel(tc, xT, w, gate, offs, out):
 
         codes_first = held.tile([P, SLOTS], U32, name="codes_first", tag="gathered_then_codes", align_bytes=64)
         quantize(x_bf_first[:].rearrange("p c t -> p (c t)"), codes_first[:], scales_first[:])
-        nc.vector.tensor_copy(
-            w_bf[0][:, 1].rearrange("p e (c i) j -> p e c j i", i=4), w_raw_1[:].rearrange("p e j (c i) -> p e c j i", i=4)
-        )
-        codes_v = held.tile([P, 2 * SLOTS], U32, name="codes_v", tag="w_raw_1_then_codes", align_bytes=64)
+        codes_v = held.tile([P, 2 * SLOTS], U32, name="codes_v", align_bytes=64)
         quantize(x_bf_v[:].rearrange("p u c t -> p (u c t)"), codes_v[:], scales_v[:])
         quantize(w_bf[0][:].rearrange("p g e n j -> p (g e n j)"), w_codes[:, 0:half], w_scales[:, 0:half])
         nc.vector.tensor_copy(

@@ -48,7 +48,7 @@ def tile_routed_moe_kernel(tc, xT, w, gate, offs, out):
         raw_for_gpsimd = held.tile([P, T], F32, name="raw_for_gpsimd", tag="raw_then_x_bf_v", align_bytes=64)
         bf_first = held.tile([P, (PACK + 1) * T], BF16, name="bf_first")
         bf_last = held.tile([P, PACK, T], BF16, name="bf_last")
-        gathered = held.tile([P, 2, PACK, SLOTS], F32, name="gathered", tag="gathered_then_codes", align_bytes=64)
+        pairs = held.tile([P, 2, 2, SLOTS * 2], BF16, name="pairs", tag="pairs_then_codes", align_bytes=64)
         x_bf_first = held.tile([P, SLOTS, PACK], BF16, name="x_bf_first", align_bytes=64)
         x_bf_last = held.tile([P, SLOTS, PACK], BF16, name="x_bf_last", align_bytes=64)
         w_raw_0 = held.tile([P, E, PACK, N], F32, name="w_raw_0")
@@ -140,7 +140,8 @@ def tile_routed_moe_kernel(tc, xT, w, gate, offs, out):
         for u, g in enumerate((FIRST_V, SECOND_V)):
             for t in range(PACK):
                 c0 = first_column(t)
-                nc.vector.tensor_copy(gathered[:, u, t, :], raw_v[g][:, c0 : c0 + WINDOW].indirect(offsets[:]))
+                pair = pairs[:, u, t // 2, :].rearrange("p (c e) -> p c e", e=2)
+                nc.vector.tensor_copy(pair[:, :, t % 2], raw_v[g][:, c0 : c0 + WINDOW].indirect(offsets[:]))
         for t in (0, 2):
             nc.scalar.copy(bf_last[:, t : t + 2, :], raw_s[SECOND_S][:, t : t + 2, :])
         for lo, hi in GROUPS:
@@ -150,12 +151,10 @@ def tile_routed_moe_kernel(tc, xT, w, gate, offs, out):
             nc.gpsimd.tensor_copy(w_bf[0][:, 0, e], w_raw_0[:, e].rearrange("p j n -> p n j"))
 
         x_bf_v = held.tile([P, 2, SLOTS, PACK], BF16, name="x_bf_v", tag="raw_then_x_bf_v", align_bytes=64)
-        nc.gpsimd.tensor_copy(x_bf_v[:, 0], gathered[:, 0].rearrange("p t c -> p c t"))
+        nc.gpsimd.tensor_copy(x_bf_v[:, 0].bitcast(F32), pairs[:, 0].bitcast(F32).rearrange("p h c -> p c h"))
         for e in range(E):
             nc.gpsimd.tensor_copy(w_bf[0][:, 1, e], w_raw_1[e][:].rearrange("p j n -> p n j"))
-        nc.vector.tensor_copy(
-            x_bf_v[:, 1].rearrange("p (c i) t -> p c t i", i=4), gathered[:, 1].rearrange("p t (c i) -> p c t i", i=4)
-        )
+        nc.vector.tensor_copy(x_bf_v[:, 1].bitcast(F32), pairs[:, 1].bitcast(F32).rearrange("p h c -> p c h"))
         half = 2 * E * N
 
 
@@ -163,7 +162,7 @@ def tile_routed_moe_kernel(tc, xT, w, gate, offs, out):
             cols = slice(half + e * 2 * N, half + (e + 1) * 2 * N)
             quantize(w_bf[1][:, e].rearrange("p g n j -> p (g n j)"), w_codes[:, cols], w_scales[:, cols])
 
-        codes_first = held.tile([P, SLOTS], U32, name="codes_first", tag="gathered_then_codes", align_bytes=64)
+        codes_first = held.tile([P, SLOTS], U32, name="codes_first", tag="pairs_then_codes", align_bytes=64)
         quantize(x_bf_first[:].rearrange("p c t -> p (c t)"), codes_first[:], scales_first[:])
         codes_v = held.tile([P, 2 * SLOTS], U32, name="codes_v", align_bytes=64)
         quantize(x_bf_v[:].rearrange("p u c t -> p (u c t)"), codes_v[:], scales_v[:])

@@ -20,8 +20,7 @@ WINDOW = 2 * T
 
 FIRST_S, FIRST_V, SECOND_V, SECOND_S = 0, 1, 2, 3
 GROUPS = ((0, 256), (256, 384), (384, 512))
-GPSIMD_PASSES = 1
-GPSIMD_PLANE = 2
+GPSIMD_PLANE = 1
 
 
 def tile_routed_moe_kernel(tc, xT, w, gate, offs, out):
@@ -29,7 +28,7 @@ def tile_routed_moe_kernel(tc, xT, w, gate, offs, out):
     mult = mybir.AluOpType.mult
     copy_fn = mybir.ActivationFunctionType.Copy
     x_planes = xT.rearrange("(g p t) n -> g p t n", p=P, t=PACK)
-    w_passes = w.rearrange("e (g p j) n -> g p e j n", p=P, j=PACK)
+    w_passes = w.rearrange("e (g p j) n -> e p g j n", p=P, j=PACK)
 
     with ExitStack() as ctx:
         lists = ctx.enter_context(tc.tile_pool(name="lists", bufs=1))
@@ -44,31 +43,30 @@ def tile_routed_moe_kernel(tc, xT, w, gate, offs, out):
         nc.scalar.activation(warm_out[:], warm[:], copy_fn)
 
         raw_v = {g: held.tile([P, (PACK + 1) * T], F32, name="raw_%d" % g) for g in (FIRST_V, SECOND_V)}
-        raw_s = {g: held.tile([P, PACK, T], F32, name="raw_%d" % g) for g in (FIRST_S, SECOND_S)}
-        raw_for_gpsimd = held.tile([P, T], F32, name="raw_for_gpsimd", tag="raw_then_x_bf_v", align_bytes=64)
+        raw_first = held.tile([P, PACK, T], F32, name="raw_first")
+        raw_last_01 = held.tile([P, 2, T], F32, name="raw_last_01")
+        raw_last_23 = held.tile([P, 2, T], F32, name="raw_last_23", tag="raw_last_23_then_x_bf", align_bytes=64)
         bf_first = held.tile([P, (PACK + 1) * T], BF16, name="bf_first")
         bf_last = held.tile([P, PACK, T], BF16, name="bf_last")
-        pairs = held.tile([P, 2, 2, SLOTS * 2], BF16, name="pairs", tag="pairs_then_codes", align_bytes=64)
+        pairs_v = held.tile([P, 2, 2, SLOTS * 2], BF16, name="pairs_v", align_bytes=64)
+        pairs_first = held.tile([P, 2, SLOTS * 2], BF16, name="pairs_first", align_bytes=64)
         x_bf_first = held.tile([P, SLOTS, PACK], BF16, name="x_bf_first", align_bytes=64)
-        x_bf_last = held.tile([P, SLOTS, PACK], BF16, name="x_bf_last", align_bytes=64)
-        w_raw_0 = held.tile([P, E, PACK, N], F32, name="w_raw_0")
-        w_raw_1 = [
-            held.tile([P, PACK, N], F32, name="w_raw_1_%d" % e, tag="w_raw_1_%d_then_codes" % e, align_bytes=64)
+        x_bf_v = held.tile([P, 2, SLOTS, PACK], BF16, name="x_bf_v", align_bytes=64)
+        x_bf_last_0 = held.tile([P, C, PACK], BF16, name="x_bf_last_0", tag="x_bf_last_0", align_bytes=64)
+        w_raw_01 = held.tile([P, 2, E, PACK, N], F32, name="w_raw_01")
+        w_raw_23 = [
+            held.tile([P, 2, PACK, N], F32, name="w_raw_23_%d" % e, tag="w_raw_23_%d" % e, align_bytes=64)
             for e in range(E)
         ]
-        w_raw_23 = held.tile([P, E, 2, PACK, N], F32, name="w_raw_23", tag="w_raw_23_then_codes", align_bytes=64)
-        w_bf = [
-            held.tile([P, 2, E, N, PACK], BF16, name="w_bf_%d" % h, tag="w_bf_%d_then_codes" % h, align_bytes=64)
-            for h in range(2)
-        ]
-        w_codes = held.tile([P, PASSES * E * N], U32, name="w_codes", align_bytes=64)
+        w_bf_01 = held.tile([P, 2, E, N, PACK], BF16, name="w_bf_01", align_bytes=64)
+        w_codes_23 = [held.tile([P, 2 * N], U32, name="w_codes_23_%d" % e, align_bytes=64) for e in range(E)]
         w_scales = held.tile([P, PASSES * E * N], U8, name="w_scales", align_bytes=64)
         scales_v = held.tile([P, 2 * SLOTS], U8, name="scales_v", align_bytes=64)
         scales_first = held.tile([P, SLOTS], U8, name="scales_first", align_bytes=64)
         scales_last = held.tile([P, SLOTS], U8, name="scales_last", align_bytes=64)
         gate_sb = held.tile([P, SLOTS], F32, name="gate_sb")
         result = held.tile([N, T], F32, name="result")
-        acc = [psum.tile([N, hi - lo], F32, name="acc_%d" % i) for i, (lo, hi) in enumerate(GROUPS)]
+        acc = {}
         sums = [
             held.tile([N, hi - lo], F32, name="sums_%d" % i, tag="sums_%d" % i, align_bytes=64)
             for i, (lo, hi) in enumerate(GROUPS)
@@ -78,17 +76,20 @@ def tile_routed_moe_kernel(tc, xT, w, gate, offs, out):
             return (PACK - 1 - t) * T
 
         def load_plane(g, t):
-            if (g, t) == (FIRST_S, GPSIMD_PLANE):
-                nc.sync.dma_start(raw_for_gpsimd[:], x_planes[g, :, t, :])
-            elif g in raw_s:
-                nc.sync.dma_start(raw_s[g][:, t, :], x_planes[g, :, t, :])
+            if g == FIRST_S:
+                nc.sync.dma_start(raw_first[:, t, :], x_planes[g, :, t, :])
+            elif g == SECOND_S:
+                nc.sync.dma_start(raw_last_01[:, t, :], x_planes[g, :, t, :])
             else:
                 nc.sync.dma_start(raw_v[g][:, first_column(t) : first_column(t) + T], x_planes[g, :, t, :])
 
+        def load_weights_01(g, e):
+            nc.sync.dma_start(w_raw_01[:, g, e], w_passes[e, :, g])
+
         vector_planes = [(g, t) for g in (FIRST_V, SECOND_V) for t in range(PACK)]
         scalar_planes = [(FIRST_S, t) for t in range(PACK)] + [(SECOND_S, 0), (SECOND_S, 1)]
-        w_blocks = [(0, 0), (0, 1), (1, 0), (1, 1)]
-        for kind in "VOSVWVSVSWVVSVWVWSS":
+        w_blocks = [(0, 0), (0, 1), (1, 0)]
+        for kind in "VOSVSVWVSVWVSWVSVS":
             if kind == "O":
                 nc.sync.dma_start(offsets[:], offs)
             elif kind == "V":
@@ -96,30 +97,38 @@ def tile_routed_moe_kernel(tc, xT, w, gate, offs, out):
             elif kind == "S":
                 load_plane(*scalar_planes.pop(0))
             else:
-                g, e = w_blocks.pop(0)
-                nc.sync.dma_start(w_raw_0[:, e] if g == 0 else w_raw_1[e][:], w_passes[g][:, e])
-        nc.sync.dma_start(raw_s[SECOND_S][:, 2:4, :], x_planes[SECOND_S, :, 2:4, :])
-        for g in (2, 3):
-            nc.sync.dma_start(w_raw_23[:, :, g - 2], w_passes[g])
+                load_weights_01(*w_blocks.pop(0))
+        nc.sync.dma_start(raw_last_23[:], x_planes[SECOND_S, :, 2:4, :])
+        load_weights_01(1, 1)
+        for e in range(E):
+            nc.sync.dma_start(w_raw_23[e][:], w_passes[e, :, 2:4])
         nc.sync.dma_start(gate_sb[:], gate)
 
         def slot_list(lo, hi):
             return offsets[:, lo // 16 : hi // 16]
 
+        def in_pair(pairs, t):
+            return pairs[:, t // 2, :].rearrange("p (c e) -> p c e", e=2)[:, :, t % 2]
+
+        def join_pairs(engine, x_bf, pairs):
+            engine.tensor_copy(x_bf.bitcast(F32), pairs.bitcast(F32).rearrange("p h c -> p c h"))
+
         def quantize(x_bf, codes, scales):
             nc.vector.quantize_mx(out=codes.bitcast(FP8X4), scales=scales, in_=x_bf)
 
         x_operands = {}
+        w_operands = {}
 
         def multiply(g, i):
             lo, hi = GROUPS[i]
+            if g == 0:
+                acc[i] = psum.tile([N, hi - lo], F32, name="acc_%d" % i, tag="acc")
             codes, scales = x_operands[(g, i)]
-            e = lo // C
-            col = (g * E + e) * N if g < 2 else (2 * E + e * 2 + g - 2) * N
+            w_codes, w_plane = w_operands[(g, lo // C)]
             nc.tensor.matmul_mx(
                 out=acc[i][:],
-                lhsT=w_codes[:, col : col + N].bitcast(FP8X4),
-                lhsT_scale=w_scales[:, col : col + N],
+                lhsT=w_codes.bitcast(FP8X4),
+                lhsT_scale=w_plane,
                 rhs=codes.bitcast(FP8X4),
                 rhs_scale=scales,
                 start=(g == 0),
@@ -130,47 +139,60 @@ def tile_routed_moe_kernel(tc, xT, w, gate, offs, out):
             lo, hi = GROUPS[i]
             nc.vector.tensor_tensor(result[:].indirect(slot_list(lo, hi)), sums[i][:], gate_sb[:, lo:hi], mult)
 
+        def interleave_weights(w_bf, raw):
+            nc.vector.tensor_copy(
+                w_bf.rearrange("p g (c i) j -> p g c j i", i=4), raw.rearrange("p g j (c i) -> p g c j i", i=4)
+            )
+
         for t in range(PACK):
             c0 = first_column(t)
             if t == GPSIMD_PLANE:
-                nc.gpsimd.tensor_copy(bf_first[:, c0 : c0 + T], raw_for_gpsimd[:])
+                nc.gpsimd.tensor_copy(bf_first[:, c0 : c0 + T], raw_first[:, t, :])
             else:
-                nc.scalar.copy(bf_first[:, c0 : c0 + T], raw_s[FIRST_S][:, t, :])
-            nc.scalar.activation(x_bf_first[:, :, t], bf_first[:, c0 : c0 + WINDOW].indirect(offsets[:]), copy_fn)
+                nc.scalar.copy(bf_first[:, c0 : c0 + T], raw_first[:, t, :])
+            nc.scalar.activation(in_pair(pairs_first, t), bf_first[:, c0 : c0 + WINDOW].indirect(offsets[:]), copy_fn)
         for u, g in enumerate((FIRST_V, SECOND_V)):
             for t in range(PACK):
                 c0 = first_column(t)
-                pair = pairs[:, u, t // 2, :].rearrange("p (c e) -> p c e", e=2)
-                nc.vector.tensor_copy(pair[:, :, t % 2], raw_v[g][:, c0 : c0 + WINDOW].indirect(offsets[:]))
-        for t in (0, 2):
-            nc.scalar.copy(bf_last[:, t : t + 2, :], raw_s[SECOND_S][:, t : t + 2, :])
-        for lo, hi in GROUPS:
+                nc.vector.tensor_copy(in_pair(pairs_v[:, u], t), raw_v[g][:, c0 : c0 + WINDOW].indirect(offsets[:]))
+        for t in (0, 1):
+            nc.scalar.copy(bf_last[:, t, :], raw_last_01[:, t, :])
+        nc.scalar.copy(bf_last[:, 2:4, :], raw_last_23[:])
+        x_bf_last_12 = held.tile([P, C, PACK], BF16, name="x_bf_last_12", tag="raw_last_23_then_x_bf", align_bytes=64)
+        x_bf_last = [x_bf_last_0[:], x_bf_last_12[:, 0 : C // 2], x_bf_last_12[:, C // 2 : C]]
+        for i, (lo, hi) in enumerate(GROUPS):
             for t in range(PACK):
-                nc.scalar.activation(x_bf_last[:, lo:hi, t], bf_last[:, t, :].indirect(slot_list(lo, hi)), copy_fn)
+                nc.scalar.activation(x_bf_last[i][:, :, t], bf_last[:, t, :].indirect(slot_list(lo, hi)), copy_fn)
         for e in range(E):
-            nc.gpsimd.tensor_copy(w_bf[0][:, 0, e], w_raw_0[:, e].rearrange("p j n -> p n j"))
+            nc.gpsimd.tensor_copy(w_bf_01[:, 0, e], w_raw_01[:, 0, e].rearrange("p j n -> p n j"))
+        join_pairs(nc.gpsimd, x_bf_v[:, 0], pairs_v[:, 0])
+        nc.gpsimd.tensor_copy(w_bf_01[:, 1, 0], w_raw_01[:, 1, 0].rearrange("p j n -> p n j"))
+        join_pairs(nc.gpsimd, x_bf_first[:], pairs_first[:])
 
-        x_bf_v = held.tile([P, 2, SLOTS, PACK], BF16, name="x_bf_v", tag="raw_then_x_bf_v", align_bytes=64)
-        nc.gpsimd.tensor_copy(x_bf_v[:, 0].bitcast(F32), pairs[:, 0].bitcast(F32).rearrange("p h c -> p c h"))
-        for e in range(E):
-            nc.gpsimd.tensor_copy(w_bf[0][:, 1, e], w_raw_1[e][:].rearrange("p j n -> p n j"))
-        nc.vector.tensor_copy(x_bf_v[:, 1].bitcast(F32), pairs[:, 1].bitcast(F32).rearrange("p h c -> p c h"))
-        half = 2 * E * N
-
-
-        def w_quantize_expert(e):
-            cols = slice(half + e * 2 * N, half + (e + 1) * 2 * N)
-            quantize(w_bf[1][:, e].rearrange("p g n j -> p (g n j)"), w_codes[:, cols], w_scales[:, cols])
-
-        codes_first = held.tile([P, SLOTS], U32, name="codes_first", tag="pairs_then_codes", align_bytes=64)
+        join_pairs(nc.vector, x_bf_v[:, 1], pairs_v[:, 1])
+        codes_first = held.tile([P, SLOTS], U32, name="codes_first", align_bytes=64)
         quantize(x_bf_first[:].rearrange("p c t -> p (c t)"), codes_first[:], scales_first[:])
         codes_v = held.tile([P, 2 * SLOTS], U32, name="codes_v", align_bytes=64)
         quantize(x_bf_v[:].rearrange("p u c t -> p (u c t)"), codes_v[:], scales_v[:])
-        quantize(w_bf[0][:].rearrange("p g e n j -> p (g e n j)"), w_codes[:, 0:half], w_scales[:, 0:half])
-        nc.vector.tensor_copy(
-            w_bf[1][:].rearrange("p e g (c i) j -> p (e g) c j i", i=4),
-            w_raw_23[:].rearrange("p e g j (c i) -> p (e g) c j i", i=4),
-        )
+        interleave_weights(w_bf_01[:, 1, 1:2], w_raw_01[:, 1, 1:2])
+        w_bf_23_0 = held.tile([P, 2, N, PACK], BF16, name="w_bf_23_0", tag="w_bf_23_0_then_codes", align_bytes=64)
+        interleave_weights(w_bf_23_0[:], w_raw_23[0][:])
+        w_codes_01 = held.tile([P, 2 * E * N], U32, name="w_codes_01", tag="w_raw_23_0", align_bytes=64)
+        half = 2 * E * N
+        quantize(w_bf_01[:].rearrange("p g e n j -> p (g e n j)"), w_codes_01[:], w_scales[:, 0:half])
+
+        for g in range(2):
+            for e in range(E):
+                col = (g * E + e) * N
+                w_operands[(g, e)] = (w_codes_01[:, col : col + N], w_scales[:, col : col + N])
+
+        def quantize_expert(e, w_bf):
+            base = half + e * 2 * N
+            quantize(w_bf.rearrange("p g n j -> p (g n j)"), w_codes_23[e][:], w_scales[:, base : base + 2 * N])
+            for u in range(2):
+                col = u * N
+                w_operands[(2 + u, e)] = (w_codes_23[e][:, col : col + N], w_scales[:, base + col : base + col + N])
+
         for i, (lo, hi) in enumerate(GROUPS):
             x_operands[(FIRST_S, i)] = (codes_first[:, lo:hi], scales_first[:, lo:hi])
             for u, g in enumerate((FIRST_V, SECOND_V)):
@@ -178,26 +200,28 @@ def tile_routed_moe_kernel(tc, xT, w, gate, offs, out):
 
         def quantize_last(i, codes):
             lo, hi = GROUPS[i]
-            quantize(x_bf_last[:, lo:hi, :].rearrange("p c t -> p (c t)"), codes, scales_last[:, lo:hi])
+            quantize(x_bf_last[i].rearrange("p c t -> p (c t)"), codes, scales_last[:, lo:hi])
             x_operands[(SECOND_S, i)] = (codes, scales_last[:, lo:hi])
-            for g in range(PASSES):
-                multiply(g, i)
 
-        codes_last_0 = held.tile([P, C], U32, name="codes_last_0", tag="w_raw_23_then_codes", align_bytes=64)
-        lo, hi = GROUPS[0]
-        quantize(x_bf_last[:, lo:hi, :].rearrange("p c t -> p (c t)"), codes_last_0[:], scales_last[:, lo:hi])
-        x_operands[(SECOND_S, 0)] = (codes_last_0[:], scales_last[:, lo:hi])
-        w_quantize_expert(0)
+        quantize_expert(0, w_bf_23_0[:])
+        codes_last_0 = held.tile([P, C], U32, name="codes_last_0", tag="w_bf_23_0_then_codes", align_bytes=64)
+        quantize_last(0, codes_last_0[:])
         for g in range(PASSES):
             multiply(g, 0)
-        w_quantize_expert(1)
+        w_bf_23_1 = held.tile([P, 2, N, PACK], BF16, name="w_bf_23_1", tag="x_bf_last_0", align_bytes=64)
+        interleave_weights(w_bf_23_1[:], w_raw_23[1][:])
         nc.vector.tensor_copy(sums[0][:], acc[0][:])
-        codes_last_1 = held.tile([P, C // 2], U32, name="codes_last_1", tag="w_raw_23_then_codes", align_bytes=64)
+        quantize_expert(1, w_bf_23_1[:])
+        codes_last_1 = held.tile([P, C // 2], U32, name="codes_last_1", tag="w_bf_23_0_then_codes", align_bytes=64)
         quantize_last(1, codes_last_1[:])
+        for g in range(PASSES):
+            multiply(g, 1)
         nc.scalar.copy(sums[1][:], acc[1][:])
         scatter(0)
         codes_last_2 = held.tile([P, C // 2], U32, name="codes_last_2", tag="sums_0", align_bytes=64)
         quantize_last(2, codes_last_2[:])
+        for g in range(PASSES):
+            multiply(g, 2)
         nc.scalar.copy(sums[2][:], acc[2][:])
         scatter(1)
         scatter(2)

@@ -20,7 +20,7 @@ WINDOW = 2 * T
 
 FIRST_S, FIRST_V, SECOND_V, SECOND_S = 0, 1, 2, 3
 GROUPS = ((0, 256), (256, 384), (384, 512))
-GPSIMD_PLANE = 1
+GPSIMD_PLANES = (1, 2)
 
 
 def tile_routed_moe_kernel(tc, xT, w, gate, offs, out):
@@ -42,7 +42,10 @@ def tile_routed_moe_kernel(tc, xT, w, gate, offs, out):
         warm_out = held.tile([P, 1], F32, name="warm_out")
         nc.scalar.activation(warm_out[:], warm[:], copy_fn)
 
-        raw_v = {g: held.tile([P, (PACK + 1) * T], F32, name="raw_%d" % g) for g in (FIRST_V, SECOND_V)}
+        raw_v = {
+            g: held.tile([P, (PACK + 1) * T], F32, name="raw_%d" % g, tag="raw_%d" % g, align_bytes=64)
+            for g in (FIRST_V, SECOND_V)
+        }
         raw_first = held.tile([P, PACK, T], F32, name="raw_first")
         raw_last_01 = held.tile([P, 2, T], F32, name="raw_last_01")
         raw_last_23 = held.tile([P, 2, T], F32, name="raw_last_23", tag="raw_last_23_then_x_bf", align_bytes=64)
@@ -51,9 +54,12 @@ def tile_routed_moe_kernel(tc, xT, w, gate, offs, out):
         pairs_v = held.tile([P, 2, 2, SLOTS * 2], BF16, name="pairs_v", align_bytes=64)
         pairs_first = held.tile([P, 2, SLOTS * 2], BF16, name="pairs_first", align_bytes=64)
         x_bf_first = held.tile([P, SLOTS, PACK], BF16, name="x_bf_first", align_bytes=64)
-        x_bf_v = held.tile([P, 2, SLOTS, PACK], BF16, name="x_bf_v", align_bytes=64)
         x_bf_last_0 = held.tile([P, C, PACK], BF16, name="x_bf_last_0", tag="x_bf_last_0", align_bytes=64)
-        w_raw_01 = held.tile([P, 2, E, PACK, N], F32, name="w_raw_01")
+        w_raw_01 = {
+            (g, e): held.tile([P, PACK, N], F32, name="w_raw_%d_%d" % (g, e), tag="w_raw_%d_%d" % (g, e), align_bytes=64)
+            for g in range(2)
+            for e in range(E)
+        }
         w_raw_23 = [
             held.tile([P, 2, PACK, N], F32, name="w_raw_23_%d" % e, tag="w_raw_23_%d" % e, align_bytes=64)
             for e in range(E)
@@ -63,9 +69,9 @@ def tile_routed_moe_kernel(tc, xT, w, gate, offs, out):
         w_scales = held.tile([P, PASSES * E * N], U8, name="w_scales", align_bytes=64)
         scales_v = held.tile([P, 2 * SLOTS], U8, name="scales_v", align_bytes=64)
         scales_first = held.tile([P, SLOTS], U8, name="scales_first", align_bytes=64)
-        scales_last = held.tile([P, SLOTS], U8, name="scales_last", align_bytes=64)
+        scales_last_0 = held.tile([P, C], U8, name="scales_last_0", tag="scales_then_x_bf", align_bytes=64)
+        scales_last_12 = held.tile([P, C], U8, name="scales_last_12", align_bytes=64)
         gate_sb = held.tile([P, SLOTS], F32, name="gate_sb")
-        result = held.tile([N, T], F32, name="result")
         acc = {}
         sums = [
             held.tile([N, hi - lo], F32, name="sums_%d" % i, tag="sums_%d" % i, align_bytes=64)
@@ -84,12 +90,12 @@ def tile_routed_moe_kernel(tc, xT, w, gate, offs, out):
                 nc.sync.dma_start(raw_v[g][:, first_column(t) : first_column(t) + T], x_planes[g, :, t, :])
 
         def load_weights_01(g, e):
-            nc.sync.dma_start(w_raw_01[:, g, e], w_passes[e, :, g])
+            nc.sync.dma_start(w_raw_01[(g, e)][:], w_passes[e, :, g])
 
         vector_planes = [(g, t) for g in (FIRST_V, SECOND_V) for t in range(PACK)]
         scalar_planes = [(FIRST_S, t) for t in range(PACK)] + [(SECOND_S, 0), (SECOND_S, 1)]
         w_blocks = [(0, 0), (0, 1), (1, 0)]
-        for kind in "VOSVSVWVSVWVSWVSVS":
+        for kind in "VOSVSVSVWVSVWSVVWS":
             if kind == "O":
                 nc.sync.dma_start(offsets[:], offs)
             elif kind == "V":
@@ -135,7 +141,7 @@ def tile_routed_moe_kernel(tc, xT, w, gate, offs, out):
                 stop=(g == PASSES - 1),
             )
 
-        def scatter(i):
+        def scatter(i, result):
             lo, hi = GROUPS[i]
             nc.vector.tensor_tensor(result[:].indirect(slot_list(lo, hi)), sums[i][:], gate_sb[:, lo:hi], mult)
 
@@ -146,7 +152,7 @@ def tile_routed_moe_kernel(tc, xT, w, gate, offs, out):
 
         for t in range(PACK):
             c0 = first_column(t)
-            if t == GPSIMD_PLANE:
+            if t in GPSIMD_PLANES:
                 nc.gpsimd.tensor_copy(bf_first[:, c0 : c0 + T], raw_first[:, t, :])
             else:
                 nc.scalar.copy(bf_first[:, c0 : c0 + T], raw_first[:, t, :])
@@ -158,23 +164,34 @@ def tile_routed_moe_kernel(tc, xT, w, gate, offs, out):
         for t in (0, 1):
             nc.scalar.copy(bf_last[:, t, :], raw_last_01[:, t, :])
         nc.scalar.copy(bf_last[:, 2:4, :], raw_last_23[:])
-        x_bf_last_12 = held.tile([P, C, PACK], BF16, name="x_bf_last_12", tag="raw_last_23_then_x_bf", align_bytes=64)
-        x_bf_last = [x_bf_last_0[:], x_bf_last_12[:, 0 : C // 2], x_bf_last_12[:, C // 2 : C]]
-        for i, (lo, hi) in enumerate(GROUPS):
+        x_bf_last_1 = held.tile([P, C // 2, PACK], BF16, name="x_bf_last_1", tag="raw_last_23_then_x_bf", align_bytes=64)
+        x_bf_last = {0: x_bf_last_0[:], 1: x_bf_last_1[:]}
+
+        def gather_last(i):
+            lo, hi = GROUPS[i]
             for t in range(PACK):
                 nc.scalar.activation(x_bf_last[i][:, :, t], bf_last[:, t, :].indirect(slot_list(lo, hi)), copy_fn)
-        for e in range(E):
-            nc.gpsimd.tensor_copy(w_bf_01[:, 0, e], w_raw_01[:, 0, e].rearrange("p j n -> p n j"))
+
+        nc.scalar.copy(
+            w_bf_01[:, 1, 1].rearrange("p (c i) j -> p c j i", i=4), w_raw_01[(1, 1)][:].rearrange("p j (c i) -> p c j i", i=4)
+        )
+        gather_last(0)
+        gather_last(1)
+        def interleave_block(g, e):
+            nc.gpsimd.tensor_copy(w_bf_01[:, g, e], w_raw_01[(g, e)][:].rearrange("p j n -> p n j"))
+
+        interleave_block(0, 0)
+        x_bf_v = held.tile([P, 2, SLOTS, PACK], BF16, name="x_bf_v", tag="w_raw_0_0", align_bytes=64)
         join_pairs(nc.gpsimd, x_bf_v[:, 0], pairs_v[:, 0])
-        nc.gpsimd.tensor_copy(w_bf_01[:, 1, 0], w_raw_01[:, 1, 0].rearrange("p j n -> p n j"))
+        interleave_block(0, 1)
         join_pairs(nc.gpsimd, x_bf_first[:], pairs_first[:])
+        interleave_block(1, 0)
 
         join_pairs(nc.vector, x_bf_v[:, 1], pairs_v[:, 1])
-        codes_first = held.tile([P, SLOTS], U32, name="codes_first", align_bytes=64)
+        codes_first = held.tile([P, SLOTS], U32, name="codes_first", tag="raw_%d" % SECOND_V, align_bytes=64)
         quantize(x_bf_first[:].rearrange("p c t -> p (c t)"), codes_first[:], scales_first[:])
         codes_v = held.tile([P, 2 * SLOTS], U32, name="codes_v", align_bytes=64)
         quantize(x_bf_v[:].rearrange("p u c t -> p (u c t)"), codes_v[:], scales_v[:])
-        interleave_weights(w_bf_01[:, 1, 1:2], w_raw_01[:, 1, 1:2])
         w_bf_23_0 = held.tile([P, 2, N, PACK], BF16, name="w_bf_23_0", tag="w_bf_23_0_then_codes", align_bytes=64)
         interleave_weights(w_bf_23_0[:], w_raw_23[0][:])
         w_codes_01 = held.tile([P, 2 * E * N], U32, name="w_codes_01", tag="w_raw_23_0", align_bytes=64)
@@ -200,30 +217,35 @@ def tile_routed_moe_kernel(tc, xT, w, gate, offs, out):
 
         def quantize_last(i, codes):
             lo, hi = GROUPS[i]
-            quantize(x_bf_last[i].rearrange("p c t -> p (c t)"), codes, scales_last[:, lo:hi])
-            x_operands[(SECOND_S, i)] = (codes, scales_last[:, lo:hi])
+            scales = scales_last_0[:] if i == 0 else scales_last_12[:, lo - C : hi - C]
+            quantize(x_bf_last[i].rearrange("p c t -> p (c t)"), codes, scales)
+            x_operands[(SECOND_S, i)] = (codes, scales)
 
         quantize_expert(0, w_bf_23_0[:])
         codes_last_0 = held.tile([P, C], U32, name="codes_last_0", tag="w_bf_23_0_then_codes", align_bytes=64)
         quantize_last(0, codes_last_0[:])
         for g in range(PASSES):
             multiply(g, 0)
+        nc.scalar.copy(sums[0][:], acc[0][:])
+        x_bf_last_2 = held.tile([P, C // 2, PACK], BF16, name="x_bf_last_2", tag="scales_then_x_bf", align_bytes=64)
+        x_bf_last[2] = x_bf_last_2[:]
+        gather_last(2)
         w_bf_23_1 = held.tile([P, 2, N, PACK], BF16, name="w_bf_23_1", tag="x_bf_last_0", align_bytes=64)
         interleave_weights(w_bf_23_1[:], w_raw_23[1][:])
-        nc.vector.tensor_copy(sums[0][:], acc[0][:])
         quantize_expert(1, w_bf_23_1[:])
         codes_last_1 = held.tile([P, C // 2], U32, name="codes_last_1", tag="w_bf_23_0_then_codes", align_bytes=64)
         quantize_last(1, codes_last_1[:])
         for g in range(PASSES):
             multiply(g, 1)
+        result = held.tile([N, T], F32, name="result", tag="x_bf_last_0", align_bytes=64)
         nc.scalar.copy(sums[1][:], acc[1][:])
-        scatter(0)
-        codes_last_2 = held.tile([P, C // 2], U32, name="codes_last_2", tag="sums_0", align_bytes=64)
+        scatter(0, result)
+        codes_last_2 = held.tile([P, C // 2], U32, name="codes_last_2", tag="w_bf_23_0_then_codes", align_bytes=64)
         quantize_last(2, codes_last_2[:])
         for g in range(PASSES):
             multiply(g, 2)
         nc.scalar.copy(sums[2][:], acc[2][:])
-        scatter(1)
-        scatter(2)
+        scatter(1, result)
+        scatter(2, result)
 
         nc.sync.dma_start(out, result[:])

@@ -69,10 +69,9 @@ def tile_routed_moe_kernel(tc, xT, w, gate, offs, out):
         w_scales = held.tile([P, PASSES * E * N], U8, name="w_scales", align_bytes=64)
         scales_v = held.tile([P, 2 * SLOTS], U8, name="scales_v", align_bytes=64)
         scales_first = held.tile([P, SLOTS], U8, name="scales_first", align_bytes=64)
-        scales_last_0 = held.tile([P, C], U8, name="scales_last_0", tag="scales_then_x_bf", align_bytes=64)
-        scales_last_12 = held.tile([P, C], U8, name="scales_last_12", align_bytes=64)
+        scales_last = held.tile([P, SLOTS], U8, name="scales_last", align_bytes=64)
         gate_sb = held.tile([P, SLOTS], F32, name="gate_sb")
-        acc = {}
+        acc = [psum.tile([N, hi - lo], F32, name="acc_%d" % i) for i, (lo, hi) in enumerate(GROUPS)]
         sums = [
             held.tile([N, hi - lo], F32, name="sums_%d" % i, tag="sums_%d" % i, align_bytes=64)
             for i, (lo, hi) in enumerate(GROUPS)
@@ -125,10 +124,8 @@ def tile_routed_moe_kernel(tc, xT, w, gate, offs, out):
         x_operands = {}
         w_operands = {}
 
-        def multiply(g, i):
+        def multiply(g, i, start, stop):
             lo, hi = GROUPS[i]
-            if g == 0:
-                acc[i] = psum.tile([N, hi - lo], F32, name="acc_%d" % i, tag="acc")
             codes, scales = x_operands[(g, i)]
             w_codes, w_plane = w_operands[(g, lo // C)]
             nc.tensor.matmul_mx(
@@ -137,9 +134,14 @@ def tile_routed_moe_kernel(tc, xT, w, gate, offs, out):
                 lhsT_scale=w_plane,
                 rhs=codes.bitcast(FP8X4),
                 rhs_scale=scales,
-                start=(g == 0),
-                stop=(g == PASSES - 1),
+                start=start,
+                stop=stop,
             )
+
+        def multiply_group(i):
+            order = (0, 1, 2, 3) if i == 0 else (3, 0, 1, 2)
+            for n, g in enumerate(order):
+                multiply(g, i, n == 0, n == PASSES - 1)
 
         def scatter(i, result):
             lo, hi = GROUPS[i]
@@ -164,8 +166,8 @@ def tile_routed_moe_kernel(tc, xT, w, gate, offs, out):
         for t in (0, 1):
             nc.scalar.copy(bf_last[:, t, :], raw_last_01[:, t, :])
         nc.scalar.copy(bf_last[:, 2:4, :], raw_last_23[:])
-        x_bf_last_1 = held.tile([P, C // 2, PACK], BF16, name="x_bf_last_1", tag="raw_last_23_then_x_bf", align_bytes=64)
-        x_bf_last = {0: x_bf_last_0[:], 1: x_bf_last_1[:]}
+        x_bf_last_12 = held.tile([P, C, PACK], BF16, name="x_bf_last_12", tag="raw_last_23_then_x_bf", align_bytes=64)
+        x_bf_last = [x_bf_last_0[:], x_bf_last_12[:, 0 : C // 2], x_bf_last_12[:, C // 2 : C]]
 
         def gather_last(i):
             lo, hi = GROUPS[i]
@@ -177,6 +179,7 @@ def tile_routed_moe_kernel(tc, xT, w, gate, offs, out):
         )
         gather_last(0)
         gather_last(1)
+        gather_last(2)
         def interleave_block(g, e):
             nc.gpsimd.tensor_copy(w_bf_01[:, g, e], w_raw_01[(g, e)][:].rearrange("p j n -> p n j"))
 
@@ -217,33 +220,27 @@ def tile_routed_moe_kernel(tc, xT, w, gate, offs, out):
 
         def quantize_last(i, codes):
             lo, hi = GROUPS[i]
-            scales = scales_last_0[:] if i == 0 else scales_last_12[:, lo - C : hi - C]
+            scales = scales_last[:, lo:hi]
             quantize(x_bf_last[i].rearrange("p c t -> p (c t)"), codes, scales)
             x_operands[(SECOND_S, i)] = (codes, scales)
 
         quantize_expert(0, w_bf_23_0[:])
         codes_last_0 = held.tile([P, C], U32, name="codes_last_0", tag="w_bf_23_0_then_codes", align_bytes=64)
         quantize_last(0, codes_last_0[:])
-        for g in range(PASSES):
-            multiply(g, 0)
-        nc.scalar.copy(sums[0][:], acc[0][:])
-        x_bf_last_2 = held.tile([P, C // 2, PACK], BF16, name="x_bf_last_2", tag="scales_then_x_bf", align_bytes=64)
-        x_bf_last[2] = x_bf_last_2[:]
-        gather_last(2)
+        multiply_group(0)
         w_bf_23_1 = held.tile([P, 2, N, PACK], BF16, name="w_bf_23_1", tag="x_bf_last_0", align_bytes=64)
         interleave_weights(w_bf_23_1[:], w_raw_23[1][:])
+        nc.vector.tensor_copy(sums[0][:], acc[0][:])
         quantize_expert(1, w_bf_23_1[:])
         codes_last_1 = held.tile([P, C // 2], U32, name="codes_last_1", tag="w_bf_23_0_then_codes", align_bytes=64)
         quantize_last(1, codes_last_1[:])
-        for g in range(PASSES):
-            multiply(g, 1)
+        multiply_group(1)
         result = held.tile([N, T], F32, name="result", tag="x_bf_last_0", align_bytes=64)
         nc.scalar.copy(sums[1][:], acc[1][:])
         scatter(0, result)
         codes_last_2 = held.tile([P, C // 2], U32, name="codes_last_2", tag="w_bf_23_0_then_codes", align_bytes=64)
         quantize_last(2, codes_last_2[:])
-        for g in range(PASSES):
-            multiply(g, 2)
+        multiply_group(2)
         nc.scalar.copy(sums[2][:], acc[2][:])
         scatter(1, result)
         scatter(2, result)

@@ -43,37 +43,37 @@ def tile_routed_moe_kernel(tc, xT, w, gate, offs, out):
         nc.scalar.activation(warm_out[:], warm[:], copy_fn)
 
         raw_v = {
-            g: held.tile([P, (PACK + 1) * T], F32, name="raw_%d" % g, tag="raw_%d" % g, align_bytes=64)
+            g: held.tile([P, (PACK + 1) * T], F32, name="raw_%d" % g, tag="raw_%d" % g, align_bytes=256)
             for g in (FIRST_V, SECOND_V)
         }
-        raw_first = held.tile([P, PACK, T], F32, name="raw_first")
-        raw_last_01 = held.tile([P, 2, T], F32, name="raw_last_01")
-        raw_last_23 = held.tile([P, 2, T], F32, name="raw_last_23", tag="raw_last_23_then_x_bf", align_bytes=64)
+        raw_first = held.tile([P, PACK, T], F32, name="raw_first", align_bytes=256)
+        raw_last_01 = held.tile([P, 2, T], F32, name="raw_last_01", align_bytes=256)
+        raw_last_23 = held.tile([P, 2, T], F32, name="raw_last_23", tag="raw_last_23_then_x_bf", align_bytes=256)
         bf_first = held.tile([P, (PACK + 1) * T], BF16, name="bf_first")
         bf_last = held.tile([P, PACK, T], BF16, name="bf_last")
-        pairs_v = held.tile([P, 2, 2, SLOTS * 2], BF16, name="pairs_v", align_bytes=64)
-        pairs_first = held.tile([P, 2, SLOTS * 2], BF16, name="pairs_first", align_bytes=64)
-        x_bf_first = held.tile([P, SLOTS, PACK], BF16, name="x_bf_first", align_bytes=64)
-        x_bf_last_0 = held.tile([P, C, PACK], BF16, name="x_bf_last_0", tag="x_bf_last_0", align_bytes=64)
+        pairs_v = held.tile([P, 2, 2, SLOTS * 2], BF16, name="pairs_v", align_bytes=256)
+        pairs_first = held.tile([P, 2, SLOTS * 2], BF16, name="pairs_first", align_bytes=256)
+        x_bf_first = held.tile([P, SLOTS, PACK], BF16, name="x_bf_first", align_bytes=256)
+        x_bf_last_0 = held.tile([P, C, PACK], BF16, name="x_bf_last_0", tag="x_bf_last_0", align_bytes=256)
         w_raw_01 = {
-            (g, e): held.tile([P, PACK, N], F32, name="w_raw_%d_%d" % (g, e), tag="w_raw_%d_%d" % (g, e), align_bytes=64)
+            (g, e): held.tile([P, PACK, N], F32, name="w_raw_%d_%d" % (g, e), tag="w_raw_%d_%d" % (g, e), align_bytes=256)
             for g in range(2)
             for e in range(E)
         }
         w_raw_23 = [
-            held.tile([P, 2, PACK, N], F32, name="w_raw_23_%d" % e, tag="w_raw_23_%d" % e, align_bytes=64)
+            held.tile([P, 2, PACK, N], F32, name="w_raw_23_%d" % e, tag="w_raw_23_%d" % e, align_bytes=256)
             for e in range(E)
         ]
-        w_bf_01 = held.tile([P, 2, E, N, PACK], BF16, name="w_bf_01", align_bytes=64)
-        w_codes_23 = [held.tile([P, 2 * N], U32, name="w_codes_23_%d" % e, align_bytes=64) for e in range(E)]
-        w_scales = held.tile([P, PASSES * E * N], U8, name="w_scales", align_bytes=64)
-        scales_v = held.tile([P, 2 * SLOTS], U8, name="scales_v", align_bytes=64)
-        scales_first = held.tile([P, SLOTS], U8, name="scales_first", align_bytes=64)
-        scales_last = held.tile([P, SLOTS], U8, name="scales_last", align_bytes=64)
-        gate_sb = held.tile([P, SLOTS], F32, name="gate_sb")
+        w_bf_01 = held.tile([P, 2, E, N, PACK], BF16, name="w_bf_01", align_bytes=256)
+        w_codes_23 = [held.tile([P, 2 * N], U32, name="w_codes_23_%d" % e, align_bytes=256) for e in range(E)]
+        w_scales = held.tile([P, PASSES * E * N], U8, name="w_scales", align_bytes=256)
+        scales_v = held.tile([P, 2 * SLOTS], U8, name="scales_v", align_bytes=256)
+        scales_first = held.tile([P, SLOTS], U8, name="scales_first", align_bytes=256)
+        scales_last = held.tile([P, SLOTS], U8, name="scales_last", align_bytes=256)
+        gate_sb = held.tile([P, SLOTS], F32, name="gate_sb", align_bytes=256)
         acc = [psum.tile([N, hi - lo], F32, name="acc_%d" % i) for i, (lo, hi) in enumerate(GROUPS)]
         sums = [
-            held.tile([N, hi - lo], F32, name="sums_%d" % i, tag="sums_%d" % i, align_bytes=64)
+            held.tile([N, hi - lo], F32, name="sums_%d" % i, tag="sums_%d" % i, align_bytes=256)
             for i, (lo, hi) in enumerate(GROUPS)
         ]
 
@@ -166,7 +166,7 @@ def tile_routed_moe_kernel(tc, xT, w, gate, offs, out):
         for t in (0, 1):
             nc.scalar.copy(bf_last[:, t, :], raw_last_01[:, t, :])
         nc.scalar.copy(bf_last[:, 2:4, :], raw_last_23[:])
-        x_bf_last_12 = held.tile([P, C, PACK], BF16, name="x_bf_last_12", tag="raw_last_23_then_x_bf", align_bytes=64)
+        x_bf_last_12 = held.tile([P, C, PACK], BF16, name="x_bf_last_12", tag="raw_last_23_then_x_bf", align_bytes=256)
         x_bf_last = [x_bf_last_0[:], x_bf_last_12[:, 0 : C // 2], x_bf_last_12[:, C // 2 : C]]
 
         def gather_last(i):
@@ -184,20 +184,20 @@ def tile_routed_moe_kernel(tc, xT, w, gate, offs, out):
             nc.gpsimd.tensor_copy(w_bf_01[:, g, e], w_raw_01[(g, e)][:].rearrange("p j n -> p n j"))
 
         interleave_block(0, 0)
-        x_bf_v = held.tile([P, 2, SLOTS, PACK], BF16, name="x_bf_v", tag="w_raw_0_0", align_bytes=64)
+        x_bf_v = held.tile([P, 2, SLOTS, PACK], BF16, name="x_bf_v", tag="w_raw_0_0", align_bytes=256)
         join_pairs(nc.gpsimd, x_bf_v[:, 0], pairs_v[:, 0])
         interleave_block(0, 1)
         join_pairs(nc.gpsimd, x_bf_first[:], pairs_first[:])
         interleave_block(1, 0)
 
         join_pairs(nc.vector, x_bf_v[:, 1], pairs_v[:, 1])
-        codes_first = held.tile([P, SLOTS], U32, name="codes_first", tag="raw_%d" % SECOND_V, align_bytes=64)
+        codes_first = held.tile([P, SLOTS], U32, name="codes_first", tag="raw_%d" % SECOND_V, align_bytes=256)
         quantize(x_bf_first[:].rearrange("p c t -> p (c t)"), codes_first[:], scales_first[:])
-        codes_v = held.tile([P, 2 * SLOTS], U32, name="codes_v", align_bytes=64)
+        codes_v = held.tile([P, 2 * SLOTS], U32, name="codes_v", align_bytes=256)
         quantize(x_bf_v[:].rearrange("p u c t -> p (u c t)"), codes_v[:], scales_v[:])
-        w_bf_23_0 = held.tile([P, 2, N, PACK], BF16, name="w_bf_23_0", tag="w_bf_23_0_then_codes", align_bytes=64)
+        w_bf_23_0 = held.tile([P, 2, N, PACK], BF16, name="w_bf_23_0", tag="w_bf_23_0_then_codes", align_bytes=256)
         interleave_weights(w_bf_23_0[:], w_raw_23[0][:])
-        w_codes_01 = held.tile([P, 2 * E * N], U32, name="w_codes_01", tag="w_raw_23_0", align_bytes=64)
+        w_codes_01 = held.tile([P, 2 * E * N], U32, name="w_codes_01", tag="w_raw_23_0", align_bytes=256)
         half = 2 * E * N
         quantize(w_bf_01[:].rearrange("p g e n j -> p (g e n j)"), w_codes_01[:], w_scales[:, 0:half])
 
@@ -225,20 +225,20 @@ def tile_routed_moe_kernel(tc, xT, w, gate, offs, out):
             x_operands[(SECOND_S, i)] = (codes, scales)
 
         quantize_expert(0, w_bf_23_0[:])
-        codes_last_0 = held.tile([P, C], U32, name="codes_last_0", tag="w_bf_23_0_then_codes", align_bytes=64)
+        codes_last_0 = held.tile([P, C], U32, name="codes_last_0", tag="w_bf_23_0_then_codes", align_bytes=256)
         quantize_last(0, codes_last_0[:])
         multiply_group(0)
-        w_bf_23_1 = held.tile([P, 2, N, PACK], BF16, name="w_bf_23_1", tag="x_bf_last_0", align_bytes=64)
+        w_bf_23_1 = held.tile([P, 2, N, PACK], BF16, name="w_bf_23_1", tag="x_bf_last_0", align_bytes=256)
         interleave_weights(w_bf_23_1[:], w_raw_23[1][:])
         nc.vector.tensor_copy(sums[0][:], acc[0][:])
         quantize_expert(1, w_bf_23_1[:])
-        codes_last_1 = held.tile([P, C // 2], U32, name="codes_last_1", tag="w_bf_23_0_then_codes", align_bytes=64)
+        codes_last_1 = held.tile([P, C // 2], U32, name="codes_last_1", tag="w_bf_23_0_then_codes", align_bytes=256)
         quantize_last(1, codes_last_1[:])
         multiply_group(1)
-        result = held.tile([N, T], F32, name="result", tag="x_bf_last_0", align_bytes=64)
+        result = held.tile([N, T], F32, name="result", tag="x_bf_last_0", align_bytes=256)
         nc.scalar.copy(sums[1][:], acc[1][:])
         scatter(0, result)
-        codes_last_2 = held.tile([P, C // 2], U32, name="codes_last_2", tag="w_bf_23_0_then_codes", align_bytes=64)
+        codes_last_2 = held.tile([P, C // 2], U32, name="codes_last_2", tag="w_bf_23_0_then_codes", align_bytes=256)
         quantize_last(2, codes_last_2[:])
         multiply_group(2)
         nc.scalar.copy(sums[2][:], acc[2][:])

@@ -53,7 +53,7 @@ def tile_routed_moe_kernel(tc, xT, w, gate, offs, out):
         bf_last = held.tile([P, PACK, T], BF16, name="bf_last")
         pairs_v = held.tile([P, 2, 2, SLOTS * 2], BF16, name="pairs_v", align_bytes=256)
         pairs_first = held.tile([P, 2, SLOTS * 2], BF16, name="pairs_first", align_bytes=256)
-        x_bf_first = held.tile([P, SLOTS, PACK], BF16, name="x_bf_first", align_bytes=256)
+        x_bf_first = held.tile([P, SLOTS, PACK], BF16, name="x_bf_first", tag="x_bf_first", align_bytes=256)
         x_bf_last_0 = held.tile([P, C, PACK], BF16, name="x_bf_last_0", tag="x_bf_last_0", align_bytes=256)
         w_raw_01 = {
             (g, e): held.tile([P, PACK, N], F32, name="w_raw_%d_%d" % (g, e), tag="w_raw_%d_%d" % (g, e), align_bytes=256)
@@ -71,7 +71,7 @@ def tile_routed_moe_kernel(tc, xT, w, gate, offs, out):
         scales_first = held.tile([P, SLOTS], U8, name="scales_first", align_bytes=256)
         scales_last = held.tile([P, SLOTS], U8, name="scales_last", align_bytes=256)
         gate_sb = held.tile([P, SLOTS], F32, name="gate_sb", align_bytes=256)
-        acc = [psum.tile([N, hi - lo], F32, name="acc_%d" % i) for i, (lo, hi) in enumerate(GROUPS)]
+        acc = {}
         sums = [
             held.tile([N, hi - lo], F32, name="sums_%d" % i, tag="sums_%d" % i, align_bytes=256)
             for i, (lo, hi) in enumerate(GROUPS)
@@ -103,8 +103,8 @@ def tile_routed_moe_kernel(tc, xT, w, gate, offs, out):
                 load_plane(*scalar_planes.pop(0))
             else:
                 load_weights_01(*w_blocks.pop(0))
-        nc.sync.dma_start(raw_last_23[:], x_planes[SECOND_S, :, 2:4, :])
         load_weights_01(1, 1)
+        nc.sync.dma_start(raw_last_23[:], x_planes[SECOND_S, :, 2:4, :])
         for e in range(E):
             nc.sync.dma_start(w_raw_23[e][:], w_passes[e, :, 2:4])
         nc.sync.dma_start(gate_sb[:], gate)
@@ -139,7 +139,9 @@ def tile_routed_moe_kernel(tc, xT, w, gate, offs, out):
             )
 
         def multiply_group(i):
-            order = (0, 1, 2, 3) if i == 0 else (3, 0, 1, 2)
+            lo, hi = GROUPS[i]
+            acc[i] = psum.tile([N, hi - lo], F32, name="acc_%d" % i, tag="acc_%d" % (i % 2))
+            order = (3, 0, 1, 2) if i == 1 else (0, 1, 2, 3)
             for n, g in enumerate(order):
                 multiply(g, i, n == 0, n == PASSES - 1)
 
@@ -184,22 +186,32 @@ def tile_routed_moe_kernel(tc, xT, w, gate, offs, out):
             nc.gpsimd.tensor_copy(w_bf_01[:, g, e], w_raw_01[(g, e)][:].rearrange("p j n -> p n j"))
 
         interleave_block(0, 0)
-        x_bf_v = held.tile([P, 2, SLOTS, PACK], BF16, name="x_bf_v", tag="w_raw_0_0", align_bytes=256)
-        join_pairs(nc.gpsimd, x_bf_v[:, 0], pairs_v[:, 0])
+        x_bf_1 = held.tile([P, SLOTS, PACK], BF16, name="x_bf_1", tag="w_raw_0_0", align_bytes=256)
+        join_pairs(nc.gpsimd, x_bf_1[:], pairs_v[:, 0])
         interleave_block(0, 1)
         join_pairs(nc.gpsimd, x_bf_first[:], pairs_first[:])
         interleave_block(1, 0)
 
-        join_pairs(nc.vector, x_bf_v[:, 1], pairs_v[:, 1])
-        codes_first = held.tile([P, SLOTS], U32, name="codes_first", tag="raw_%d" % SECOND_V, align_bytes=256)
-        quantize(x_bf_first[:].rearrange("p c t -> p (c t)"), codes_first[:], scales_first[:])
-        codes_v = held.tile([P, 2 * SLOTS], U32, name="codes_v", align_bytes=256)
-        quantize(x_bf_v[:].rearrange("p u c t -> p (u c t)"), codes_v[:], scales_v[:])
-        w_bf_23_0 = held.tile([P, 2, N, PACK], BF16, name="w_bf_23_0", tag="w_bf_23_0_then_codes", align_bytes=256)
-        interleave_weights(w_bf_23_0[:], w_raw_23[0][:])
-        w_codes_01 = held.tile([P, 2 * E * N], U32, name="w_codes_01", tag="w_raw_23_0", align_bytes=256)
+        codes_01 = held.tile([P, 2 * SLOTS], U32, name="codes_01", tag="w_raw_1_0", align_bytes=256)
+        codes_first = codes_01[:, 0:SLOTS]
+        quantize(x_bf_first[:].rearrange("p c t -> p (c t)"), codes_first, scales_first[:])
+
+        def quantize_v(u, x_bf, codes):
+            scales = scales_v[:, u * SLOTS : (u + 1) * SLOTS]
+            quantize(x_bf.rearrange("p c t -> p (c t)"), codes, scales)
+            for i, (lo, hi) in enumerate(GROUPS):
+                x_operands[((FIRST_V, SECOND_V)[u], i)] = (codes[:, lo:hi], scales[:, lo:hi])
+
+        quantize_v(0, x_bf_1[:], codes_01[:, SLOTS : 2 * SLOTS])
+        x_bf_2 = held.tile([P, SLOTS, PACK], BF16, name="x_bf_2", tag="x_bf_first", align_bytes=256)
+        join_pairs(nc.vector, x_bf_2[:], pairs_v[:, 1])
+        w_codes_01 = held.tile([P, 2 * E * N], U32, name="w_codes_01", align_bytes=256)
         half = 2 * E * N
         quantize(w_bf_01[:].rearrange("p g e n j -> p (g e n j)"), w_codes_01[:], w_scales[:, 0:half])
+        w_bf_23_0 = held.tile([P, 2, N, PACK], BF16, name="w_bf_23_0", tag="w_bf_23_0_then_codes", align_bytes=256)
+        interleave_weights(w_bf_23_0[:], w_raw_23[0][:])
+        codes_2 = held.tile([P, SLOTS], U32, name="codes_2", tag="w_raw_23_0", align_bytes=256)
+        quantize_v(1, x_bf_2[:], codes_2[:])
 
         for g in range(2):
             for e in range(E):
@@ -215,8 +227,6 @@ def tile_routed_moe_kernel(tc, xT, w, gate, offs, out):
 
         for i, (lo, hi) in enumerate(GROUPS):
             x_operands[(FIRST_S, i)] = (codes_first[:, lo:hi], scales_first[:, lo:hi])
-            for u, g in enumerate((FIRST_V, SECOND_V)):
-                x_operands[(g, i)] = (codes_v[:, u * SLOTS + lo : u * SLOTS + hi], scales_v[:, u * SLOTS + lo : u * SLOTS + hi])
 
         def quantize_last(i, codes):
             lo, hi = GROUPS[i]

from contextlib import ExitStack

import concourse.mybir as mybir

K, T, E, C, N = 2048, 512, 2, 256, 128
FLOPS = 2 * K * N * E * C

F32 = mybir.dt.float32
BF16 = mybir.dt.bfloat16
U32 = mybir.dt.uint32
U16 = mybir.dt.uint16
U8 = mybir.dt.uint8
FP8X4 = mybir.dt.float8_e4m3fn_x4

P = 128
PACK = 4
PASSES = K // (P * PACK)
SLOTS = E * C
WINDOW = 2 * T

FIRST_S, FIRST_V, SECOND_V, SECOND_S = 0, 1, 2, 3
GROUPS = ((0, 256), (256, 384), (384, 512))
GPSIMD_PLANES = (1, 2)


def tile_routed_moe_kernel(tc, xT, w, gate, offs, out):
    nc = tc.nc
    mult = mybir.AluOpType.mult
    copy_fn = mybir.ActivationFunctionType.Copy
    x_planes = xT.rearrange("(g p t) n -> g p t n", p=P, t=PACK)
    w_passes = w.rearrange("e (g p j) n -> e p g j n", p=P, j=PACK)

    with ExitStack() as ctx:
        lists = ctx.enter_context(tc.tile_pool(name="lists", bufs=1))
        held = ctx.enter_context(tc.tile_pool(name="held", bufs=1))
        psum = ctx.enter_context(tc.psum_pool(name="psum", bufs=1))

        offsets = lists.tile([P, SLOTS // 16], U16, name="offsets")

        warm = held.tile([P, 1], F32, name="warm")
        nc.vector.memset(warm[:], 0.0)
        warm_out = held.tile([P, 1], F32, name="warm_out")
        nc.scalar.activation(warm_out[:], warm[:], copy_fn)

        raw_v = {
            g: held.tile([P, (PACK + 1) * T], F32, name="raw_%d" % g, tag="raw_%d" % g, align_bytes=256)
            for g in (FIRST_V, SECOND_V)
        }
        raw_first = held.tile([P, PACK, T], F32, name="raw_first", align_bytes=256)
        raw_last_01 = held.tile([P, 2, T], F32, name="raw_last_01", align_bytes=256)
        raw_last_23 = held.tile([P, 2, T], F32, name="raw_last_23", tag="raw_last_23_then_x_bf", align_bytes=256)
        bf_first = held.tile([P, (PACK + 1) * T], BF16, name="bf_first")
        bf_last = held.tile([P, PACK, T], BF16, name="bf_last")
        pairs_v = held.tile([P, 2, 2, SLOTS * 2], BF16, name="pairs_v", align_bytes=256)
        pairs_first = held.tile([P, 2, SLOTS * 2], BF16, name="pairs_first", align_bytes=256)
        x_bf_first = held.tile([P, SLOTS, PACK], BF16, name="x_bf_first", tag="x_bf_first", align_bytes=256)
        x_bf_last_0 = held.tile([P, C, PACK], BF16, name="x_bf_last_0", tag="x_bf_last_0", align_bytes=256)
        w_raw_01 = {
            (g, e): held.tile([P, PACK, N], F32, name="w_raw_%d_%d" % (g, e), tag="w_raw_%d_%d" % (g, e), align_bytes=256)
            for g in range(2)
            for e in range(E)
        }
        w_raw_23 = [
            held.tile([P, 2, PACK, N], F32, name="w_raw_23_%d" % e, tag="w_raw_23_%d" % e, align_bytes=256)
            for e in range(E)
        ]
        w_bf_01 = held.tile([P, 2, E, N, PACK], BF16, name="w_bf_01", align_bytes=256)
        w_codes_23 = [held.tile([P, 2 * N], U32, name="w_codes_23_%d" % e, align_bytes=256) for e in range(E)]
        w_scales = held.tile([P, PASSES * E * N], U8, name="w_scales", align_bytes=256)
        scales_v = held.tile([P, 2 * SLOTS], U8, name="scales_v", align_bytes=256)
        scales_first = held.tile([P, SLOTS], U8, name="scales_first", align_bytes=256)
        scales_last = held.tile([P, SLOTS], U8, name="scales_last", align_bytes=256)
        gate_sb = held.tile([P, SLOTS], F32, name="gate_sb", align_bytes=256)
        acc = {}
        sums = [
            held.tile([N, hi - lo], F32, name="sums_%d" % i, tag="sums_%d" % i, align_bytes=256)
            for i, (lo, hi) in enumerate(GROUPS)
        ]

        def first_column(t):
            return (PACK - 1 - t) * T

        def load_plane(g, t):
            if g == FIRST_S:
                nc.sync.dma_start(raw_first[:, t, :], x_planes[g, :, t, :])
            elif g == SECOND_S:
                nc.sync.dma_start(raw_last_01[:, t, :], x_planes[g, :, t, :])
            else:
                nc.sync.dma_start(raw_v[g][:, first_column(t) : first_column(t) + T], x_planes[g, :, t, :])

        def load_weights_01(g, e):
            nc.sync.dma_start(w_raw_01[(g, e)][:], w_passes[e, :, g])

        vector_planes = [(g, t) for g in (FIRST_V, SECOND_V) for t in range(PACK)]
        scalar_planes = [(FIRST_S, t) for t in range(PACK)] + [(SECOND_S, 0), (SECOND_S, 1)]
        w_blocks = [(0, 0), (0, 1), (1, 0)]
        for kind in "VOSVSVSVWVSVWSVVWS":
            if kind == "O":
                nc.sync.dma_start(offsets[:], offs)
            elif kind == "V":
                load_plane(*vector_planes.pop(0))
            elif kind == "S":
                load_plane(*scalar_planes.pop(0))
            else:
                load_weights_01(*w_blocks.pop(0))
        load_weights_01(1, 1)
        nc.sync.dma_start(raw_last_23[:], x_planes[SECOND_S, :, 2:4, :])
        for e in range(E):
            nc.sync.dma_start(w_raw_23[e][:], w_passes[e, :, 2:4])
        nc.sync.dma_start(gate_sb[:], gate)

        def slot_list(lo, hi):
            return offsets[:, lo // 16 : hi // 16]

        def in_pair(pairs, t):
            return pairs[:, t // 2, :].rearrange("p (c e) -> p c e", e=2)[:, :, t % 2]

        def join_pairs(engine, x_bf, pairs):
            engine.tensor_copy(x_bf.bitcast(F32), pairs.bitcast(F32).rearrange("p h c -> p c h"))

        def quantize(x_bf, codes, scales):
            nc.vector.quantize_mx(out=codes.bitcast(FP8X4), scales=scales, in_=x_bf)

        x_operands = {}
        w_operands = {}

        def multiply(g, i, start, stop):
            lo, hi = GROUPS[i]
            codes, scales = x_operands[(g, i)]
            w_codes, w_plane = w_operands[(g, lo // C)]
            nc.tensor.matmul_mx(
                out=acc[i][:],
                lhsT=w_codes.bitcast(FP8X4),
                lhsT_scale=w_plane,
                rhs=codes.bitcast(FP8X4),
                rhs_scale=scales,
                start=start,
                stop=stop,
            )

        def multiply_group(i):
            lo, hi = GROUPS[i]
            acc[i] = psum.tile([N, hi - lo], F32, name="acc_%d" % i, tag="acc_%d" % (i % 2))
            order = (3, 0, 1, 2) if i == 1 else (0, 1, 2, 3)
            for n, g in enumerate(order):
                multiply(g, i, n == 0, n == PASSES - 1)

        def scatter(i, result):
            lo, hi = GROUPS[i]
            nc.vector.tensor_tensor(result[:].indirect(slot_list(lo, hi)), sums[i][:], gate_sb[:, lo:hi], mult)

        def interleave_weights(w_bf, raw):
            nc.vector.tensor_copy(
                w_bf.rearrange("p g (c i) j -> p g c j i", i=4), raw.rearrange("p g j (c i) -> p g c j i", i=4)
            )

        for t in range(PACK):
            c0 = first_column(t)
            if t in GPSIMD_PLANES:
                nc.gpsimd.tensor_copy(bf_first[:, c0 : c0 + T], raw_first[:, t, :])
            else:
                nc.scalar.copy(bf_first[:, c0 : c0 + T], raw_first[:, t, :])
            nc.scalar.activation(in_pair(pairs_first, t), bf_first[:, c0 : c0 + WINDOW].indirect(offsets[:]), copy_fn)
        for u, g in enumerate((FIRST_V, SECOND_V)):
            for t in range(PACK):
                c0 = first_column(t)
                nc.vector.tensor_copy(in_pair(pairs_v[:, u], t), raw_v[g][:, c0 : c0 + WINDOW].indirect(offsets[:]))
        for t in (0, 1):
            nc.scalar.copy(bf_last[:, t, :], raw_last_01[:, t, :])
        nc.scalar.copy(bf_last[:, 2:4, :], raw_last_23[:])
        x_bf_last_12 = held.tile([P, C, PACK], BF16, name="x_bf_last_12", tag="raw_last_23_then_x_bf", align_bytes=256)
        x_bf_last = [x_bf_last_0[:], x_bf_last_12[:, 0 : C // 2], x_bf_last_12[:, C // 2 : C]]

        def gather_last(i):
            lo, hi = GROUPS[i]
            for t in range(PACK):
                nc.scalar.activation(x_bf_last[i][:, :, t], bf_last[:, t, :].indirect(slot_list(lo, hi)), copy_fn)

        nc.scalar.copy(
            w_bf_01[:, 1, 1].rearrange("p (c i) j -> p c j i", i=4), w_raw_01[(1, 1)][:].rearrange("p j (c i) -> p c j i", i=4)
        )
        gather_last(0)
        gather_last(1)
        gather_last(2)
        def interleave_block(g, e):
            nc.gpsimd.tensor_copy(w_bf_01[:, g, e], w_raw_01[(g, e)][:].rearrange("p j n -> p n j"))

        interleave_block(0, 0)
        x_bf_1 = held.tile([P, SLOTS, PACK], BF16, name="x_bf_1", tag="w_raw_0_0", align_bytes=256)
        join_pairs(nc.gpsimd, x_bf_1[:], pairs_v[:, 0])
        interleave_block(0, 1)
        join_pairs(nc.gpsimd, x_bf_first[:], pairs_first[:])
        interleave_block(1, 0)

        codes_01 = held.tile([P, 2 * SLOTS], U32, name="codes_01", tag="w_raw_1_0", align_bytes=256)
        codes_first = codes_01[:, 0:SLOTS]
        quantize(x_bf_first[:].rearrange("p c t -> p (c t)"), codes_first, scales_first[:])

        def quantize_v(u, x_bf, codes):
            scales = scales_v[:, u * SLOTS : (u + 1) * SLOTS]
            quantize(x_bf.rearrange("p c t -> p (c t)"), codes, scales)
            for i, (lo, hi) in enumerate(GROUPS):
                x_operands[((FIRST_V, SECOND_V)[u], i)] = (codes[:, lo:hi], scales[:, lo:hi])

        quantize_v(0, x_bf_1[:], codes_01[:, SLOTS : 2 * SLOTS])
        x_bf_2 = held.tile([P, SLOTS, PACK], BF16, name="x_bf_2", tag="x_bf_first", align_bytes=256)
        join_pairs(nc.vector, x_bf_2[:], pairs_v[:, 1])
        w_codes_01 = held.tile([P, 2 * E * N], U32, name="w_codes_01", align_bytes=256)
        half = 2 * E * N
        quantize(w_bf_01[:].rearrange("p g e n j -> p (g e n j)"), w_codes_01[:], w_scales[:, 0:half])
        w_bf_23_0 = held.tile([P, 2, N, PACK], BF16, name="w_bf_23_0", tag="w_bf_23_0_then_codes", align_bytes=256)
        interleave_weights(w_bf_23_0[:], w_raw_23[0][:])
        codes_2 = held.tile([P, SLOTS], U32, name="codes_2", tag="w_raw_23_0", align_bytes=256)
        quantize_v(1, x_bf_2[:], codes_2[:])

        for g in range(2):
            for e in range(E):
                col = (g * E + e) * N
                w_operands[(g, e)] = (w_codes_01[:, col : col + N], w_scales[:, col : col + N])

        def quantize_expert(e, w_bf):
            base = half + e * 2 * N
            quantize(w_bf.rearrange("p g n j -> p (g n j)"), w_codes_23[e][:], w_scales[:, base : base + 2 * N])
            for u in range(2):
                col = u * N
                w_operands[(2 + u, e)] = (w_codes_23[e][:, col : col + N], w_scales[:, base + col : base + col + N])

        for i, (lo, hi) in enumerate(GROUPS):
            x_operands[(FIRST_S, i)] = (codes_first[:, lo:hi], scales_first[:, lo:hi])

        def quantize_last(i, codes):
            lo, hi = GROUPS[i]
            scales = scales_last[:, lo:hi]
            quantize(x_bf_last[i].rearrange("p c t -> p (c t)"), codes, scales)
            x_operands[(SECOND_S, i)] = (codes, scales)

        quantize_expert(0, w_bf_23_0[:])
        codes_last_0 = held.tile([P, C], U32, name="codes_last_0", tag="w_bf_23_0_then_codes", align_bytes=256)
        quantize_last(0, codes_last_0[:])
        multiply_group(0)
        w_bf_23_1 = held.tile([P, 2, N, PACK], BF16, name="w_bf_23_1", tag="x_bf_last_0", align_bytes=256)
        interleave_weights(w_bf_23_1[:], w_raw_23[1][:])
        nc.vector.tensor_copy(sums[0][:], acc[0][:])
        quantize_expert(1, w_bf_23_1[:])
        codes_last_1 = held.tile([P, C // 2], U32, name="codes_last_1", tag="w_bf_23_0_then_codes", align_bytes=256)
        quantize_last(1, codes_last_1[:])
        multiply_group(1)
        result = held.tile([N, T], F32, name="result", tag="x_bf_last_0", align_bytes=256)
        nc.scalar.copy(sums[1][:], acc[1][:])
        scatter(0, result)
        codes_last_2 = held.tile([P, C // 2], U32, name="codes_last_2", tag="w_bf_23_0_then_codes", align_bytes=256)
        quantize_last(2, codes_last_2[:])
        multiply_group(2)
        nc.scalar.copy(sums[2][:], acc[2][:])
        scatter(1, result)
        scatter(2, result)

        nc.sync.dma_start(out, result[:])
